import numpy as np
import ml_dtypes


def mxq(x, axis, fmt="e4m3"):
    dtype, down = {"e4m3": (ml_dtypes.float8_e4m3fn, 7), "e5m2": (ml_dtypes.float8_e5m2, 14)}[fmt]
    v = np.moveaxis(np.asarray(x, np.float32).astype(ml_dtypes.bfloat16).astype(np.float64), axis, -1)
    blocks = v.reshape(v.shape[:-1] + (-1, 32))
    amax = np.abs(blocks).max(-1, keepdims=True)
    byte = np.maximum(np.where(amax > 0, np.frexp(amax)[1] - 1 + 127, 0) - down, 1)
    scale = np.exp2(byte - 127.0)
    codes = (blocks / scale).astype(np.float32).astype(dtype).astype(np.float64)
    return np.moveaxis((codes * scale).reshape(v.shape), -1, axis)


WIDE = False


def mx_kscale(k):
    if not WIDE:
        return np.ones(k)
    levels = np.array([10, -10, 5, -5, 0])
    if k % 512:
        return np.exp2(np.random.permutation(np.resize(levels, k // 32))).repeat(32)
    a = np.empty((k // 512, 16))
    for p in range(k // 512):
        a[p, :8] = np.random.permutation(np.resize(levels, 8))
        for g in range(8):
            far = levels[np.abs(levels - a[p, g]) >= 10]
            a[p, g + 8] = far[np.random.randint(len(far))]
    return np.exp2(a.ravel()).repeat(32)


def f64(x):
    return np.asarray(x).astype(np.float64)


def striped(idx):
    return np.tile(np.asarray(idx).reshape(-1, 16).T, (8, 1)).astype(np.uint16)


def unstriped(offs):
    return offs[:16].T.reshape(-1).astype(np.int64)


E2M1 = np.array([0.0, 0.5, 1.0, 1.5, 2.0, 3.0, 4.0, 6.0, -0.0, -0.5, -1.0, -1.5, -2.0, -3.0, -4.0, -6.0])


def pack_weight(w, fmt):
    k, n = w.shape
    w = f64(np.asarray(w, np.float32).astype(ml_dtypes.bfloat16)).reshape(k // 32, 32, n)
    amax = np.abs(w).max(1)
    if fmt == "e4m3":
        byte = np.frexp(amax)[1] - 1 + 127 - 7
    else:
        mant, ex = np.frexp(amax / 6.0)
        byte = np.where(mant > 0.5, ex, ex - 1) + 127
    byte = np.clip(np.where(amax > 0, byte, 1), 1, 254)
    scaled = (w * np.exp2(127.0 - byte)[:, None, :]).reshape(k, n).astype(np.float32)
    by_word = np.ascontiguousarray(scaled.reshape(k // 512, 128, 4, n).transpose(0, 1, 3, 2))
    if fmt == "e4m3":
        words = by_word.astype(ml_dtypes.float8_e4m3fn).view(np.uint8)
    else:
        c = by_word.astype(ml_dtypes.float4_e2m1fn).view(np.uint8) & 0xF
        words = (c[..., 0::2] | (c[..., 1::2] << 4)).reshape(k // 512, 128, 2 * n)
    return np.ascontiguousarray(words), np.ascontiguousarray(byte.astype(np.uint8).reshape(k // 512, 16, n))


def unpack_weight(words, scales, fmt):
    g, _, n = scales.shape
    words = np.ascontiguousarray(words).reshape(g, 128, n, -1)
    if fmt == "e4m3":
        vals = words.view(ml_dtypes.float8_e4m3fn).astype(np.float64)
    else:
        nib = np.empty((g, 128, n, 4), np.uint8)
        nib[..., 0::2] = words & 0xF
        nib[..., 1::2] = words >> 4
        vals = E2M1[nib]
    vals = vals * np.repeat(np.exp2(scales.astype(np.float64) - 127.0), 8, axis=1)[..., None]
    return vals.transpose(0, 1, 3, 2).reshape(g * 512, n)


B, N, T, D, DV, NQ = 1, 1536, 4096, 1024, 128, 256
PAGE = 512
CAP = 2.0


def setup_inputs():
    n = np.random.standard_normal
    pages = np.random.permutation(T // PAGE)[:B * N // PAGE]
    idx = (pages[:, None] * PAGE + np.arange(PAGE)[None, :]).reshape(-1)
    s = mx_kscale(D)[:, None]
    u = np.ones(T)
    u[idx] = mx_kscale(B * N)
    r = np.random.uniform(0.5, 2.0, T)
    qp = [pack_weight(x, "e4m3") for x in n((B, D, NQ)) * s * (0.80 / np.sqrt(D))]
    k = n((D, T)) / s
    v = n((DV, T)) / (u * r)
    kp = pack_weight(k, "e2m1")
    vp = pack_weight(v.T, "e4m3")
    return {
        "q_words": np.stack([x[0] for x in qp]),
        "q_scales": np.stack([x[1] for x in qp]),
        "k_words": np.ascontiguousarray(kp[0].reshape(D // 1024, 2, 128, T, 2).transpose(0, 2, 3, 1, 4)).reshape(D // 1024, 128, T, 4),
        "k_scales": kp[1],
        "v_words": vp[0],
        "v_scales": vp[1],
        "vs": np.tile(u * r, (128, 1)).astype(np.float32),
        "sink": (2.0 + 3.0 * n((B, NQ, 1))).astype(np.float32),
        "offs": striped(idx),
        "voffs": striped((pages[:, None] * DV + np.arange(DV)[None, :]).reshape(-1)),
    }


def reference(q_words, q_scales, k_words, k_scales, v_words, v_scales, vs, sink, offs, voffs):
    idx = unstriped(offs)
    k = unpack_weight(k_words.reshape(D // 1024, 128, T, 2, 2).transpose(0, 3, 1, 2, 4).reshape(D // 512, 128, 2 * T), k_scales, "e2m1")
    v = unpack_weight(v_words, v_scales, "e4m3")
    v = v.reshape(T // 512, 512, DV)[unstriped(voffs)[::DV] // DV].reshape(B, N, DV)
    pick = lambda x: x[:, idx].reshape(x.shape[0], B, N).transpose(1, 0, 2)
    q = np.stack([unpack_weight(q_words[b], q_scales[b], "e4m3") for b in range(B)])
    score = q.transpose(0, 2, 1) @ pick(k)
    score = CAP * np.tanh(score / CAP)
    m = np.maximum(score.max(-1, keepdims=True), f64(sink))
    p = np.exp(score - m)
    total = p.sum(-1, keepdims=True) + np.exp(f64(sink) - m)
    w = p * pick(f64(vs))[:, :1, :]
    y = mxq(w, 2, "e4m3") @ v
    y = y / total
    return y

@@ -1,0 +1,203 @@
+from contextlib import ExitStack
+
+import concourse.mybir as mybir
+from concourse.masks import make_identity
+
+N, T, D, DV, NQ = 1536, 4096, 1024, 128, 256
+PAGE = 512
+CAP = 2.0
+P = 128
+PAGES = N // PAGE
+PASSES = D // 512
+QT = NQ // P
+POOL_PAGES = T // PAGE
+FLOPS = 2 * NQ * N * (D + DV)
+
+F32 = mybir.dt.float32
+BF16 = mybir.dt.bfloat16
+I32 = mybir.dt.int32
+U32 = mybir.dt.uint32
+U16 = mybir.dt.uint16
+U8 = mybir.dt.uint8
+FP8X4 = mybir.dt.float8_e4m3fn_x4
+FP4X4 = mybir.dt.float4_e2m1fn_x4
+ALU = mybir.AluOpType
+ACT = mybir.ActivationFunctionType
+AX = mybir.AxisListType
+
+
+def tile_attend_pkv4q_soft_cap_sink_kernel(
+    tc, q_words, q_scales, k_words, k_scales, v_words, v_scales, vs, sink, offs, voffs, out
+):
+    nc = tc.nc
+    with ExitStack() as ctx:
+        keep = ctx.enter_context(tc.tile_pool(name="keep", bufs=1))
+        ring = ctx.enter_context(tc.tile_pool(name="ring", bufs=3))
+        ps_s = ctx.enter_context(tc.psum_pool(name="ps_s", bufs=4))
+        ps_t = ctx.enter_context(tc.psum_pool(name="ps_t", bufs=2))
+        ps_o = ctx.enter_context(tc.psum_pool(name="ps_o", bufs=1))
+
+        offs_sb = keep.tile([P, N // 16], U16, name="offs_sb")
+        voffs_sb = keep.tile([P, PAGES * DV // 16], U16, name="voffs_sb")
+        ks_win = keep.tile([P, T], U8, name="ks_win", align_bytes=64)
+        vs_win = keep.tile([P, T], F32, name="vs_win", align_bytes=64)
+        kw_win = keep.tile([P, T], I32, name="kw_win", align_bytes=64)
+        vw_win = keep.tile([P, POOL_PAGES * DV], I32, name="vw_win", align_bytes=64)
+        vsc_win = keep.tile([P, POOL_PAGES * DV], U8, name="vsc_win", align_bytes=64)
+        qw = keep.tile([P, PASSES * NQ], I32, name="qw", align_bytes=64)
+        qs = keep.tile([P, PASSES * NQ], U8, name="qs", align_bytes=64)
+        k_planes = keep.tile([P, PASSES * N], U8, name="k_planes", align_bytes=64)
+        sink_sb = keep.tile([P, QT], F32, name="sink_sb")
+        ident = keep.tile([P, P], F32, name="ident", align_bytes=64)
+        warm = keep.tile([P, 1], F32, name="warm")
+
+        nc.gpsimd.memset(warm[:], 0.0)
+        nc.vector.memset(qs[:].bitcast(I32), 0)
+        nc.vector.memset(ks_win[0:96, :].bitcast(I32), 0)
+        nc.vector.memset(vs_win[0:127, 0:3072], 0.0)
+        nc.gpsimd.memset(vs_win[0:127, 3072:T], 0.0)
+        nc.gpsimd.memset(k_planes[:].bitcast(I32), 0)
+        nc.gpsimd.memset(vsc_win[:].bitcast(I32), 0)
+        make_identity(nc, ident[:])
+
+        nc.sync.dma_start(offs_sb[:], offs)
+        nc.sync.dma_start(ks_win[96:P, :].bitcast(I32), k_scales.rearrange("o f t -> f o t").bitcast(I32))
+        nc.sync.dma_start(vs_win[127:P, :], vs[0:1, :])
+        nc.sync.dma_start(voffs_sb[:], voffs)
+        nc.sync.dma_start(kw_win[:], k_words[0].rearrange("g t b -> g (t b)").bitcast(I32))
+        for quad in range(4):
+            nc.scalar.dma_start(
+                qs[32 * quad : 32 * quad + 4, :].bitcast(I32).rearrange("f (o q) -> f o q", o=PASSES),
+                q_scales[0, :, 4 * quad : 4 * quad + 4, :].rearrange("o f q -> f o q").bitcast(I32),
+            )
+        nc.sync.dma_start(
+            qw[:].rearrange("g (o q) -> g o q", o=PASSES),
+            q_words[0].rearrange("o g q r -> g o (q r)").bitcast(I32),
+        )
+        with nc.allow_non_contiguous_dma(reason="one logit a partition"):
+            nc.sync.dma_start(sink_sb[:], sink[0].rearrange("(c p) o -> p (c o)", p=P))
+        nc.sync.dma_start(
+            vw_win[:].rearrange("g (u e) -> g u e", u=POOL_PAGES),
+            v_words.rearrange("u g e r -> g u (e r)").bitcast(I32),
+        )
+        for quad in range(4):
+            nc.sync.dma_start(
+                vsc_win[32 * quad : 32 * quad + 4, :].bitcast(I32).rearrange("f (u e) -> f u e", u=POOL_PAGES),
+                v_scales[:, 4 * quad : 4 * quad + 4, :].rearrange("u f e -> f u e").bitcast(I32),
+            )
+        nc.scalar.activation(warm[:], warm[:], ACT.Exp)
+
+        ks_g = keep.tile([P, N], U8, name="ks_g", align_bytes=64)
+        nc.vector.tensor_copy(ks_g[:], ks_win[:].indirect(offs_sb[:]))
+        for quad in range(4):
+            nc.scalar.dma_start(
+                k_planes[32 * quad : 32 * quad + 4, :].bitcast(I32).rearrange("f (o n) -> f o n", o=PASSES),
+                ks_g[96 + 8 * quad : 96 + 8 * quad + 8, :].bitcast(I32),
+            )
+
+        vs_g = keep.tile([P, N], F32, name="vs_g", align_bytes=64)
+        nc.vector.tensor_copy(vs_g[:], vs_win[:].indirect(offs_sb[:]))
+        vs_col = []
+        for u in range(PAGES):
+            col = keep.tile([P, 4], F32, name=f"vs_col{u}")
+            nc.sync.dma_start(col[:], vs_g[127:P, u * PAGE : (u + 1) * PAGE])
+            vs_col.append(col)
+
+        th = [keep.tile([P, N + 8], F32, name=f"th{c}", tag=f"th{c}", align_bytes=64) for c in range(QT)]
+        for c in range(QT):
+            nc.scalar.activation(th[c][:, N : N + 1], sink_sb[:, c : c + 1], ACT.Copy, scale=1.0 / CAP)
+
+        for u in range(PAGES):
+            kg = ring.tile([P, PAGE], U32, name="kg", align_bytes=64, bufs=2)
+            nc.vector.tensor_copy(kg[:], kw_win[:].bitcast(U32).indirect(offs_sb[:, u * PAGE // 16 : (u + 1) * PAGE // 16]))
+            kp = ring.tile([P, PASSES * PAGE], U16, name="kp", align_bytes=64)
+            nc.vector.tensor_copy(
+                kp[:].rearrange("p (o c i) -> p c o i", o=PASSES, i=8),
+                kg[:].bitcast(U16).rearrange("p (c i o) -> p c o i", o=PASSES, i=8),
+            )
+            for c in range(QT):
+                s = ps_s.tile([P, PAGE], F32, name="s")
+                for o in range(PASSES):
+                    qc = slice(o * NQ + c * P, o * NQ + (c + 1) * P)
+                    nc.tensor.matmul_mx(
+                        out=s[:],
+                        lhsT=qw[:, qc].bitcast(FP8X4),
+                        lhsT_scale=qs[:, qc],
+                        rhs=kp[:, o * PAGE : (o + 1) * PAGE].bitcast(FP4X4),
+                        rhs_scale=k_planes[:, o * N + u * PAGE : o * N + (u + 1) * PAGE],
+                        start=(o == 0),
+                        stop=(o == PASSES - 1),
+                    )
+                nc.scalar.activation(
+                    th[c][:, u * PAGE : (u + 1) * PAGE].rearrange("p (t s) -> p t s", t=4),
+                    s[:].rearrange("p (s t) -> p t s", t=4),
+                    ACT.Tanh,
+                    scale=1.0 / CAP,
+                )
+
+        neg_c = [keep.tile([P, N + 8], F32, name=f"neg_c{c}", align_bytes=64) for c in range(QT)]
+        neg_m = [keep.tile([P, PAGES], F32, name=f"neg_m{c}") for c in range(QT)]
+
+        def cols(u):
+            return slice(u * PAGE, (u + 1) * PAGE + (1 if u == PAGES - 1 else 0))
+
+        for c in range(QT):
+            for u in range(PAGES):
+                nc.vector.tensor_scalar(
+                    neg_c[c][:, cols(u)],
+                    th[c][:, cols(u)],
+                    -CAP,
+                    neg_m[c][:, u - 1 : u] if u else None,
+                    ALU.mult,
+                    ALU.min,
+                    accum_out=neg_m[c][:, u : u + 1],
+                )
+
+        vw_g = keep.tile([P, PAGES * DV], U32, name="vw_g", tag="th0", align_bytes=64)
+        nc.vector.tensor_copy(vw_g[:], vw_win[:].bitcast(U32).indirect(voffs_sb[:]))
+        vsc_g = keep.tile([P, PAGES * DV], U8, name="vsc_g", tag="th1", align_bytes=64)
+        nc.vector.tensor_copy(vsc_g[:], vsc_win[:].indirect(voffs_sb[:]))
+
+        for c in range(QT):
+            p = keep.tile([P, N + 8], F32, name=f"p{c}", align_bytes=64)
+            part = keep.tile([P, PAGES], F32, name=f"part{c}")
+            acc = ps_o.tile([P, DV], F32, name=f"acc{c}")
+            for u in range(PAGES):
+                nc.scalar.activation(
+                    p[:, cols(u)],
+                    neg_c[c][:, cols(u)],
+                    ACT.Exp,
+                    bias=neg_m[c][:, PAGES - 1 : PAGES],
+                    scale=-1.0,
+                    accum_out=part[:, u : u + 1],
+                )
+            for u in range(PAGES):
+                pt = ps_t.tile([P, PAGE], F32, name="pt")
+                for t in range(4):
+                    nc.tensor.transpose(pt[:, t * P : (t + 1) * P], p[:, u * PAGE + t * P : u * PAGE + (t + 1) * P], ident[:])
+                w = ring.tile([P, PAGE], BF16, name="w", align_bytes=64)
+                nc.vector.tensor_tensor(
+                    w[:].rearrange("p (q t) -> p q t", t=4),
+                    pt[:].rearrange("p (t q) -> p q t", t=4),
+                    vs_col[u][:].unsqueeze(1).to_broadcast([P, P, 4]),
+                    ALU.mult,
+                )
+                wq = ring.tile([P, P], U32, name="wq", align_bytes=64)
+                ws = ring.tile([P, P], U8, name="ws", align_bytes=64)
+                nc.vector.quantize_mx(out=wq[:].bitcast(FP8X4), scales=ws[:], in_=w[:])
+                nc.tensor.matmul_mx(
+                    out=acc[:],
+                    lhsT=wq[:].bitcast(FP8X4),
+                    lhsT_scale=ws[:],
+                    rhs=vw_g[:, u * DV : (u + 1) * DV].bitcast(FP8X4),
+                    rhs_scale=vsc_g[:, u * DV : (u + 1) * DV],
+                    start=(u == 0),
+                    stop=(u == PAGES - 1),
+                )
+            total = keep.tile([P, 1], F32, name=f"total{c}")
+            nc.vector.tensor_reduce(total[:], part[:], AX.X, ALU.add)
+            inv = keep.tile([P, 1], F32, name=f"inv{c}")
+            nc.vector.reciprocal(inv[:], total[:])
+            y = keep.tile([P, DV], F32, name=f"y{c}", align_bytes=64)
+            nc.scalar.activation(y[:], acc[:], ACT.Copy, scale=inv[:])
+            nc.sync.dma_start(out[0, c * P : (c + 1) * P, :], y[:])

@@ -33,16 +33,15 @@ def tile_attend_pkv4q_soft_cap_sink_kernel(
     with ExitStack() as ctx:
         keep = ctx.enter_context(tc.tile_pool(name="keep", bufs=1))
         ring = ctx.enter_context(tc.tile_pool(name="ring", bufs=3))
-        ps_s = ctx.enter_context(tc.psum_pool(name="ps_s", bufs=4))
-        ps_t = ctx.enter_context(tc.psum_pool(name="ps_t", bufs=2))
+        ps_s = ctx.enter_context(tc.psum_pool(name="ps_s", bufs=3))
+        ps_t = ctx.enter_context(tc.psum_pool(name="ps_t", bufs=3))
         ps_o = ctx.enter_context(tc.psum_pool(name="ps_o", bufs=1))
 
         offs_sb = keep.tile([P, N // 16], U16, name="offs_sb")
         voffs_sb = keep.tile([P, PAGES * DV // 16], U16, name="voffs_sb")
-        ks_win = keep.tile([P, T], U8, name="ks_win", align_bytes=64)
+        ks_win = keep.tile([P, T], U8, name="ks_win", tag="ks_win", align_bytes=64)
         vs_win = keep.tile([P, T], F32, name="vs_win", align_bytes=64)
         kw_win = keep.tile([P, T], I32, name="kw_win", align_bytes=64)
-        vw_win = keep.tile([P, POOL_PAGES * DV], I32, name="vw_win", align_bytes=64)
         vsc_win = keep.tile([P, POOL_PAGES * DV], U8, name="vsc_win", align_bytes=64)
         qw = keep.tile([P, PASSES * NQ], I32, name="qw", align_bytes=64)
         qs = keep.tile([P, PASSES * NQ], U8, name="qs", align_bytes=64)
@@ -52,13 +51,13 @@ def tile_attend_pkv4q_soft_cap_sink_kernel(
         warm = keep.tile([P, 1], F32, name="warm")
 
         nc.gpsimd.memset(warm[:], 0.0)
-        nc.vector.memset(qs[:].bitcast(I32), 0)
+        nc.gpsimd.memset(qs[:].bitcast(I32), 0)
         nc.vector.memset(ks_win[0:96, :].bitcast(I32), 0)
-        nc.vector.memset(vs_win[0:127, 0:3072], 0.0)
-        nc.gpsimd.memset(vs_win[0:127, 3072:T], 0.0)
+        make_identity(nc, ident[:])
+        for piece in range(4):
+            nc.gpsimd.memset(vs_win[0:127, piece * 1024 : (piece + 1) * 1024], 0.0)
         nc.gpsimd.memset(k_planes[:].bitcast(I32), 0)
         nc.gpsimd.memset(vsc_win[:].bitcast(I32), 0)
-        make_identity(nc, ident[:])
 
         nc.sync.dma_start(offs_sb[:], offs)
         nc.sync.dma_start(ks_win[96:P, :].bitcast(I32), k_scales.rearrange("o f t -> f o t").bitcast(I32))
@@ -76,15 +75,6 @@ def tile_attend_pkv4q_soft_cap_sink_kernel(
         )
         with nc.allow_non_contiguous_dma(reason="one logit a partition"):
             nc.sync.dma_start(sink_sb[:], sink[0].rearrange("(c p) o -> p (c o)", p=P))
-        nc.sync.dma_start(
-            vw_win[:].rearrange("g (u e) -> g u e", u=POOL_PAGES),
-            v_words.rearrange("u g e r -> g u (e r)").bitcast(I32),
-        )
-        for quad in range(4):
-            nc.sync.dma_start(
-                vsc_win[32 * quad : 32 * quad + 4, :].bitcast(I32).rearrange("f (u e) -> f u e", u=POOL_PAGES),
-                v_scales[:, 4 * quad : 4 * quad + 4, :].rearrange("u f e -> f u e").bitcast(I32),
-            )
         nc.scalar.activation(warm[:], warm[:], ACT.Exp)
 
         ks_g = keep.tile([P, N], U8, name="ks_g", align_bytes=64)
@@ -95,17 +85,35 @@ def tile_attend_pkv4q_soft_cap_sink_kernel(
                 ks_g[96 + 8 * quad : 96 + 8 * quad + 8, :].bitcast(I32),
             )
 
-        vs_g = keep.tile([P, N], F32, name="vs_g", align_bytes=64)
-        nc.vector.tensor_copy(vs_g[:], vs_win[:].indirect(offs_sb[:]))
-        vs_col = []
-        for u in range(PAGES):
-            col = keep.tile([P, 4], F32, name=f"vs_col{u}")
-            nc.sync.dma_start(col[:], vs_g[127:P, u * PAGE : (u + 1) * PAGE])
-            vs_col.append(col)
+        vw_win = keep.tile([P, POOL_PAGES * DV], I32, name="vw_win", tag="ks_win", align_bytes=64)
+        nc.sync.dma_start(
+            vw_win[:].rearrange("g (u e) -> g u e", u=POOL_PAGES),
+            v_words.rearrange("u g e r -> g u (e r)").bitcast(I32),
+        )
+        for quad in range(4):
+            nc.sync.dma_start(
+                vsc_win[32 * quad : 32 * quad + 4, :].bitcast(I32).rearrange("f (u e) -> f u e", u=POOL_PAGES),
+                v_scales[:, 4 * quad : 4 * quad + 4, :].rearrange("u f e -> f u e").bitcast(I32),
+            )
 
-        th = [keep.tile([P, N + 8], F32, name=f"th{c}", tag=f"th{c}", align_bytes=64) for c in range(QT)]
+        def token_scales(u, tag):
+            vs_g = keep.tile([P, PAGE], F32, name=f"vs_g{u}", tag=tag, align_bytes=64)
+            nc.vector.tensor_copy(vs_g[:], vs_win[:].indirect(offs_sb[:, u * PAGE // 16 : (u + 1) * PAGE // 16]))
+            col = keep.tile([P, 4], F32, name=f"vs_col{u}")
+            nc.sync.dma_start(col[:], vs_g[127:P, :])
+            return col
+
+        vs_col = [token_scales(u, f"vs_g{u}") for u in range(PAGES - 1)]
+
+        def width(u):
+            return PAGE + (1 if u == PAGES - 1 else 0)
+
+        th = [
+            [keep.tile([P, PAGE + 8], F32, name=f"th{c}{u}", tag=f"th{c}{u}", align_bytes=64) for u in range(PAGES)]
+            for c in range(QT)
+        ]
         for c in range(QT):
-            nc.scalar.activation(th[c][:, N : N + 1], sink_sb[:, c : c + 1], ACT.Copy, scale=1.0 / CAP)
+            nc.scalar.activation(th[c][PAGES - 1][:, PAGE : PAGE + 1], sink_sb[:, c : c + 1], ACT.Copy, scale=1.0 / CAP)
 
         for u in range(PAGES):
             kg = ring.tile([P, PAGE], U32, name="kg", align_bytes=64, bufs=2)
@@ -129,7 +137,7 @@ def tile_attend_pkv4q_soft_cap_sink_kernel(
                         stop=(o == PASSES - 1),
                     )
                 nc.scalar.activation(
-                    th[c][:, u * PAGE : (u + 1) * PAGE].rearrange("p (t s) -> p t s", t=4),
+                    th[c][u][:, 0:PAGE].rearrange("p (t s) -> p t s", t=4),
                     s[:].rearrange("p (s t) -> p t s", t=4),
                     ACT.Tanh,
                     scale=1.0 / CAP,
@@ -138,14 +146,11 @@ def tile_attend_pkv4q_soft_cap_sink_kernel(
         neg_c = [keep.tile([P, N + 8], F32, name=f"neg_c{c}", align_bytes=64) for c in range(QT)]
         neg_m = [keep.tile([P, PAGES], F32, name=f"neg_m{c}") for c in range(QT)]
 
-        def cols(u):
-            return slice(u * PAGE, (u + 1) * PAGE + (1 if u == PAGES - 1 else 0))
-
         for c in range(QT):
             for u in range(PAGES):
                 nc.vector.tensor_scalar(
-                    neg_c[c][:, cols(u)],
-                    th[c][:, cols(u)],
+                    neg_c[c][:, u * PAGE : u * PAGE + width(u)],
+                    th[c][u][:, 0 : width(u)],
                     -CAP,
                     neg_m[c][:, u - 1 : u] if u else None,
                     ALU.mult,
@@ -153,24 +158,24 @@ def tile_attend_pkv4q_soft_cap_sink_kernel(
                     accum_out=neg_m[c][:, u : u + 1],
                 )
 
-        vw_g = keep.tile([P, PAGES * DV], U32, name="vw_g", tag="th0", align_bytes=64)
+        vs_col.append(token_scales(PAGES - 1, "th02"))
+        vw_g = keep.tile([P, PAGES * DV], U32, name="vw_g", tag="th12", align_bytes=64)
         nc.vector.tensor_copy(vw_g[:], vw_win[:].bitcast(U32).indirect(voffs_sb[:]))
-        vsc_g = keep.tile([P, PAGES * DV], U8, name="vsc_g", tag="th1", align_bytes=64)
+        vsc_g = keep.tile([P, PAGES * DV], U8, name="vsc_g", tag="th11", align_bytes=64)
         nc.vector.tensor_copy(vsc_g[:], vsc_win[:].indirect(voffs_sb[:]))
 
         for c in range(QT):
             p = keep.tile([P, N + 8], F32, name=f"p{c}", align_bytes=64)
-            part = keep.tile([P, PAGES], F32, name=f"part{c}")
+            total = keep.tile([P, 1], F32, name=f"total{c}")
             acc = ps_o.tile([P, DV], F32, name=f"acc{c}")
-            for u in range(PAGES):
-                nc.scalar.activation(
-                    p[:, cols(u)],
-                    neg_c[c][:, cols(u)],
-                    ACT.Exp,
-                    bias=neg_m[c][:, PAGES - 1 : PAGES],
-                    scale=-1.0,
-                    accum_out=part[:, u : u + 1],
-                )
+            nc.scalar.activation(
+                p[:, 0 : N + 1],
+                neg_c[c][:, 0 : N + 1],
+                ACT.Exp,
+                bias=neg_m[c][:, PAGES - 1 : PAGES],
+                scale=-1.0,
+                accum_out=total[:],
+            )
             for u in range(PAGES):
                 pt = ps_t.tile([P, PAGE], F32, name="pt")
                 for t in range(4):
@@ -194,8 +199,6 @@ def tile_attend_pkv4q_soft_cap_sink_kernel(
                     start=(u == 0),
                     stop=(u == PAGES - 1),
                 )
-            total = keep.tile([P, 1], F32, name=f"total{c}")
-            nc.vector.tensor_reduce(total[:], part[:], AX.X, ALU.add)
             inv = keep.tile([P, 1], F32, name=f"inv{c}")
             nc.vector.reciprocal(inv[:], total[:])
             y = keep.tile([P, DV], F32, name=f"y{c}", align_bytes=64)

@@ -33,8 +33,8 @@ def tile_attend_pkv4q_soft_cap_sink_kernel(
     with ExitStack() as ctx:
         keep = ctx.enter_context(tc.tile_pool(name="keep", bufs=1))
         ring = ctx.enter_context(tc.tile_pool(name="ring", bufs=3))
-        ps_s = ctx.enter_context(tc.psum_pool(name="ps_s", bufs=3))
-        ps_t = ctx.enter_context(tc.psum_pool(name="ps_t", bufs=3))
+        late = ctx.enter_context(tc.tile_pool(name="late", bufs=1))
+        ps_w = ctx.enter_context(tc.psum_pool(name="ps_w", bufs=6))
         ps_o = ctx.enter_context(tc.psum_pool(name="ps_o", bufs=1))
 
         offs_sb = keep.tile([P, N // 16], U16, name="offs_sb")
@@ -96,22 +96,22 @@ def tile_attend_pkv4q_soft_cap_sink_kernel(
                 v_scales[:, 4 * quad : 4 * quad + 4, :].rearrange("u f e -> f u e").bitcast(I32),
             )
 
-        def token_scales(u, tag):
-            vs_g = keep.tile([P, PAGE], F32, name=f"vs_g{u}", tag=tag, align_bytes=64)
+        def token_scales(u, vs_g):
             nc.vector.tensor_copy(vs_g[:], vs_win[:].indirect(offs_sb[:, u * PAGE // 16 : (u + 1) * PAGE // 16]))
             col = keep.tile([P, 4], F32, name=f"vs_col{u}")
             nc.sync.dma_start(col[:], vs_g[127:P, :])
             return col
 
-        vs_col = [token_scales(u, f"vs_g{u}") for u in range(PAGES - 1)]
+        vs_col = [token_scales(u, keep.tile([P, PAGE], F32, name=f"vs_g{u}", align_bytes=64)) for u in range(PAGES - 1)]
 
         def width(u):
             return PAGE + (1 if u == PAGES - 1 else 0)
 
         th = [
-            [keep.tile([P, PAGE + 8], F32, name=f"th{c}{u}", tag=f"th{c}{u}", align_bytes=64) for u in range(PAGES)]
+            [keep.tile([P, PAGE + 8], F32, name=f"th{c}{u}", align_bytes=64) if (c, u) != (QT - 1, PAGES - 1) else None for u in range(PAGES)]
             for c in range(QT)
         ]
+        th[QT - 1][PAGES - 1] = late.tile([P, PAGE + 8], F32, name="th_last", align_bytes=64, offset=2048)
         for c in range(QT):
             nc.scalar.activation(th[c][PAGES - 1][:, PAGE : PAGE + 1], sink_sb[:, c : c + 1], ACT.Copy, scale=1.0 / CAP)
 
@@ -124,7 +124,7 @@ def tile_attend_pkv4q_soft_cap_sink_kernel(
                 kg[:].bitcast(U16).rearrange("p (c i o) -> p c o i", o=PASSES, i=8),
             )
             for c in range(QT):
-                s = ps_s.tile([P, PAGE], F32, name="s")
+                s = ps_w.tile([P, PAGE], F32, name="s", tag="bank")
                 for o in range(PASSES):
                     qc = slice(o * NQ + c * P, o * NQ + (c + 1) * P)
                     nc.tensor.matmul_mx(
@@ -158,49 +158,78 @@ def tile_attend_pkv4q_soft_cap_sink_kernel(
                     accum_out=neg_m[c][:, u : u + 1],
                 )
 
-        vs_col.append(token_scales(PAGES - 1, "th02"))
-        vw_g = keep.tile([P, PAGES * DV], U32, name="vw_g", tag="th12", align_bytes=64)
+        vs_col.append(token_scales(PAGES - 1, late.tile([P, PAGE], F32, name="vs_g_last", align_bytes=64, offset=64)))
+        vw_g = late.tile([P, PAGES * DV], U32, name="vw_g", align_bytes=64, offset=2112)
         nc.vector.tensor_copy(vw_g[:], vw_win[:].bitcast(U32).indirect(voffs_sb[:]))
-        vsc_g = keep.tile([P, PAGES * DV], U8, name="vsc_g", tag="th11", align_bytes=64)
+        vsc_g = late.tile([P, PAGES * DV], U8, name="vsc_g", align_bytes=64, offset=3648)
         nc.vector.tensor_copy(vsc_g[:], vsc_win[:].indirect(voffs_sb[:]))
 
+        p = [[None] * PAGES for c in range(QT)]
+        part = keep.tile([P, QT, PAGES], F32, name="part")
         for c in range(QT):
-            p = keep.tile([P, N + 8], F32, name=f"p{c}", align_bytes=64)
-            total = keep.tile([P, 1], F32, name=f"total{c}")
-            acc = ps_o.tile([P, DV], F32, name=f"acc{c}")
-            nc.scalar.activation(
-                p[:, 0 : N + 1],
-                neg_c[c][:, 0 : N + 1],
-                ACT.Exp,
-                bias=neg_m[c][:, PAGES - 1 : PAGES],
-                scale=-1.0,
-                accum_out=total[:],
-            )
             for u in range(PAGES):
-                pt = ps_t.tile([P, PAGE], F32, name="pt")
-                for t in range(4):
-                    nc.tensor.transpose(pt[:, t * P : (t + 1) * P], p[:, u * PAGE + t * P : u * PAGE + (t + 1) * P], ident[:])
-                w = ring.tile([P, PAGE], BF16, name="w", align_bytes=64)
-                nc.vector.tensor_tensor(
-                    w[:].rearrange("p (q t) -> p q t", t=4),
-                    pt[:].rearrange("p (t q) -> p q t", t=4),
-                    vs_col[u][:].unsqueeze(1).to_broadcast([P, P, 4]),
-                    ALU.mult,
+                p[c][u] = keep.tile([P, PAGE + 8], F32, name=f"p{c}{u}", tag=f"p{c}{u}", align_bytes=64)
+                nc.scalar.activation(
+                    p[c][u][:, 0 : width(u)],
+                    neg_c[c][:, u * PAGE : u * PAGE + width(u)],
+                    ACT.Exp,
+                    bias=neg_m[c][:, PAGES - 1 : PAGES],
+                    scale=-1.0,
+                    accum_out=part[:, c, u : u + 1],
                 )
-                wq = ring.tile([P, P], U32, name="wq", align_bytes=64)
-                ws = ring.tile([P, P], U8, name="ws", align_bytes=64)
-                nc.vector.quantize_mx(out=wq[:].bitcast(FP8X4), scales=ws[:], in_=w[:])
+        total = keep.tile([P, QT], F32, name="total")
+        nc.vector.tensor_reduce(total[:], part[:], AX.X, ALU.add)
+        inv = keep.tile([P, QT], F32, name="inv")
+        nc.vector.reciprocal(inv[:], total[:])
+
+        w = [keep.tile([P, N], BF16, name=f"w{c}", align_bytes=64) for c in range(QT)]
+        for c in range(QT):
+            for u in range(PAGES):
+                pt = ps_w.tile([P, PAGE], F32, name="pt", tag="bank")
+                for t in range(4):
+                    nc.tensor.transpose(pt[:, t * P : (t + 1) * P], p[c][u][:, t * P : (t + 1) * P], ident[:])
+                w_page = w[c][:, u * PAGE : (u + 1) * PAGE]
+                if c == 0:
+                    nc.vector.tensor_tensor(
+                        w_page.rearrange("p (q t) -> p q t", t=4),
+                        pt[:].rearrange("p (t q) -> p q t", t=4),
+                        vs_col[u][:].unsqueeze(1).to_broadcast([P, P, 4]),
+                        ALU.mult,
+                    )
+                else:
+                    flat = ring.tile([P, PAGE], BF16, name="flat", align_bytes=64)
+                    for t in range(4):
+                        nc.scalar.activation(
+                            flat[:, t * P : (t + 1) * P],
+                            pt[:, t * P : (t + 1) * P],
+                            ACT.Copy,
+                            scale=vs_col[u][:, t : t + 1],
+                        )
+                    nc.vector.tensor_copy(
+                        w_page.rearrange("p (g i t) -> p g t i", i=4, t=4),
+                        flat[:].rearrange("p (t g i) -> p g t i", i=4, t=4),
+                    )
+
+        for c in range(QT):
+            wq = keep.tile([P, PAGES * P], U32, name=f"wq{c}", align_bytes=64)
+            ws = keep.tile([P, PAGES * P], U8, name=f"ws{c}", tag="p12" if c == 0 else "ws1", align_bytes=64)
+            for lo, hi in ((0, 2), (2, 3)):
+                nc.vector.quantize_mx(
+                    out=wq[:, lo * P : hi * P].bitcast(FP8X4),
+                    scales=ws[:, lo * P : hi * P],
+                    in_=w[c][:, lo * PAGE : hi * PAGE],
+                )
+            acc = ps_o.tile([P, DV], F32, name=f"acc{c}")
+            for u in range(PAGES):
                 nc.tensor.matmul_mx(
                     out=acc[:],
-                    lhsT=wq[:].bitcast(FP8X4),
-                    lhsT_scale=ws[:],
+                    lhsT=wq[:, u * P : (u + 1) * P].bitcast(FP8X4),
+                    lhsT_scale=ws[:, u * P : (u + 1) * P],
                     rhs=vw_g[:, u * DV : (u + 1) * DV].bitcast(FP8X4),
                     rhs_scale=vsc_g[:, u * DV : (u + 1) * DV],
                     start=(u == 0),
                     stop=(u == PAGES - 1),
                 )
-            inv = keep.tile([P, 1], F32, name=f"inv{c}")
-            nc.vector.reciprocal(inv[:], total[:])
             y = keep.tile([P, DV], F32, name=f"y{c}", align_bytes=64)
-            nc.scalar.activation(y[:], acc[:], ACT.Copy, scale=inv[:])
+            nc.scalar.activation(y[:], acc[:], ACT.Copy, scale=inv[:, c : c + 1])
             nc.sync.dma_start(out[0, c * P : (c + 1) * P, :], y[:])

@@ -34,75 +34,68 @@ def tile_attend_pkv4q_soft_cap_sink_kernel(
         keep = ctx.enter_context(tc.tile_pool(name="keep", bufs=1))
         ring = ctx.enter_context(tc.tile_pool(name="ring", bufs=3))
         late = ctx.enter_context(tc.tile_pool(name="late", bufs=1))
+        mid = ctx.enter_context(tc.tile_pool(name="mid", bufs=1))
         ps_w = ctx.enter_context(tc.psum_pool(name="ps_w", bufs=6))
         ps_o = ctx.enter_context(tc.psum_pool(name="ps_o", bufs=1))
 
         offs_sb = keep.tile([P, N // 16], U16, name="offs_sb")
         voffs_sb = keep.tile([P, PAGES * DV // 16], U16, name="voffs_sb")
         ks_win = keep.tile([P, T], U8, name="ks_win", tag="ks_win", align_bytes=64)
-        vs_win = keep.tile([P, T], F32, name="vs_win", align_bytes=64)
         kw_win = keep.tile([P, T], I32, name="kw_win", align_bytes=64)
         vsc_win = keep.tile([P, POOL_PAGES * DV], U8, name="vsc_win", align_bytes=64)
         qw = keep.tile([P, PASSES * NQ], I32, name="qw", align_bytes=64)
-        qs = keep.tile([P, PASSES * NQ], U8, name="qs", align_bytes=64)
         k_planes = keep.tile([P, PASSES * N], U8, name="k_planes", align_bytes=64)
         sink_sb = keep.tile([P, QT], F32, name="sink_sb")
         ident = keep.tile([P, P], F32, name="ident", align_bytes=64)
         warm = keep.tile([P, 1], F32, name="warm")
 
-        nc.gpsimd.memset(warm[:], 0.0)
-        nc.gpsimd.memset(qs[:].bitcast(I32), 0)
-        nc.vector.memset(ks_win[0:96, :].bitcast(I32), 0)
-        make_identity(nc, ident[:])
-        for piece in range(4):
-            nc.gpsimd.memset(vs_win[0:127, piece * 1024 : (piece + 1) * 1024], 0.0)
-        nc.gpsimd.memset(k_planes[:].bitcast(I32), 0)
         nc.gpsimd.memset(vsc_win[:].bitcast(I32), 0)
+        nc.gpsimd.memset(warm[:], 0.0)
+        make_identity(nc, ident[:])
+        nc.vector.memset(ks_win[0:96, :].bitcast(I32), 0)
+        nc.vector.memset(k_planes[:].bitcast(I32), 0)
 
         nc.sync.dma_start(offs_sb[:], offs)
         nc.sync.dma_start(ks_win[96:P, :].bitcast(I32), k_scales.rearrange("o f t -> f o t").bitcast(I32))
-        nc.sync.dma_start(vs_win[127:P, :], vs[0:1, :])
         nc.sync.dma_start(voffs_sb[:], voffs)
         nc.sync.dma_start(kw_win[:], k_words[0].rearrange("g t b -> g (t b)").bitcast(I32))
-        for quad in range(4):
-            nc.scalar.dma_start(
-                qs[32 * quad : 32 * quad + 4, :].bitcast(I32).rearrange("f (o q) -> f o q", o=PASSES),
-                q_scales[0, :, 4 * quad : 4 * quad + 4, :].rearrange("o f q -> f o q").bitcast(I32),
-            )
         nc.sync.dma_start(
             qw[:].rearrange("g (o q) -> g o q", o=PASSES),
             q_words[0].rearrange("o g q r -> g o (q r)").bitcast(I32),
         )
         with nc.allow_non_contiguous_dma(reason="one logit a partition"):
             nc.sync.dma_start(sink_sb[:], sink[0].rearrange("(c p) o -> p (c o)", p=P))
+        for quad in range(4):
+            nc.scalar.dma_start(
+                vsc_win[32 * quad : 32 * quad + 4, :].bitcast(I32).rearrange("f (u e) -> f u e", u=POOL_PAGES),
+                v_scales[:, 4 * quad : 4 * quad + 4, :].rearrange("u f e -> f u e").bitcast(I32),
+            )
         nc.scalar.activation(warm[:], warm[:], ACT.Exp)
 
-        ks_g = keep.tile([P, N], U8, name="ks_g", align_bytes=64)
+        ks_g = mid.tile([P, N], U8, name="ks_g", align_bytes=64, offset=4 * T - N // 2)
         nc.vector.tensor_copy(ks_g[:], ks_win[:].indirect(offs_sb[:]))
         for quad in range(4):
             nc.scalar.dma_start(
                 k_planes[32 * quad : 32 * quad + 4, :].bitcast(I32).rearrange("f (o n) -> f o n", o=PASSES),
                 ks_g[96 + 8 * quad : 96 + 8 * quad + 8, :].bitcast(I32),
             )
+        qs = keep.tile([P, PASSES * NQ], U8, name="qs", tag="ks_win", align_bytes=64)
+        nc.vector.memset(qs[:].bitcast(I32), 0)
+        for quad in range(4):
+            nc.sync.dma_start(
+                qs[32 * quad : 32 * quad + 4, :].bitcast(I32).rearrange("f (o q) -> f o q", o=PASSES),
+                q_scales[0, :, 4 * quad : 4 * quad + 4, :].rearrange("o f q -> f o q").bitcast(I32),
+            )
+        vsc_g = keep.tile([P, PAGES * DV], U8, name="vsc_g", align_bytes=64)
+        nc.vector.tensor_copy(vsc_g[:], vsc_win[:].indirect(voffs_sb[:]))
 
-        vw_win = keep.tile([P, POOL_PAGES * DV], I32, name="vw_win", tag="ks_win", align_bytes=64)
+        vs_win = mid.tile([P, T], F32, name="vs_win", align_bytes=64, offset=0)
+        nc.sync.dma_start(vs_win[:], vs)
+        vw_win = mid.tile([P, POOL_PAGES * DV], I32, name="vw_win", align_bytes=64, offset=4 * T)
         nc.sync.dma_start(
             vw_win[:].rearrange("g (u e) -> g u e", u=POOL_PAGES),
             v_words.rearrange("u g e r -> g u (e r)").bitcast(I32),
         )
-        for quad in range(4):
-            nc.sync.dma_start(
-                vsc_win[32 * quad : 32 * quad + 4, :].bitcast(I32).rearrange("f (u e) -> f u e", u=POOL_PAGES),
-                v_scales[:, 4 * quad : 4 * quad + 4, :].rearrange("u f e -> f u e").bitcast(I32),
-            )
-
-        def token_scales(u, vs_g):
-            nc.vector.tensor_copy(vs_g[:], vs_win[:].indirect(offs_sb[:, u * PAGE // 16 : (u + 1) * PAGE // 16]))
-            col = keep.tile([P, 4], F32, name=f"vs_col{u}")
-            nc.sync.dma_start(col[:], vs_g[127:P, :])
-            return col
-
-        vs_col = [token_scales(u, keep.tile([P, PAGE], F32, name=f"vs_g{u}", align_bytes=64)) for u in range(PAGES - 1)]
 
         def width(u):
             return PAGE + (1 if u == PAGES - 1 else 0)
@@ -111,7 +104,7 @@ def tile_attend_pkv4q_soft_cap_sink_kernel(
             [keep.tile([P, PAGE + 8], F32, name=f"th{c}{u}", align_bytes=64) if (c, u) != (QT - 1, PAGES - 1) else None for u in range(PAGES)]
             for c in range(QT)
         ]
-        th[QT - 1][PAGES - 1] = late.tile([P, PAGE + 8], F32, name="th_last", align_bytes=64, offset=2048)
+        th[QT - 1][PAGES - 1] = late.tile([P, PAGE + 8], F32, name="th_last", align_bytes=64, offset=4 * N - 64)
         for c in range(QT):
             nc.scalar.activation(th[c][PAGES - 1][:, PAGE : PAGE + 1], sink_sb[:, c : c + 1], ACT.Copy, scale=1.0 / CAP)
 
@@ -158,11 +151,16 @@ def tile_attend_pkv4q_soft_cap_sink_kernel(
                     accum_out=neg_m[c][:, u : u + 1],
                 )
 
-        vs_col.append(token_scales(PAGES - 1, late.tile([P, PAGE], F32, name="vs_g_last", align_bytes=64, offset=64)))
-        vw_g = late.tile([P, PAGES * DV], U32, name="vw_g", align_bytes=64, offset=2112)
+        vs_first = keep.tile([P, PAGE], F32, name="vs_first", align_bytes=64)
+        vs_rest = late.tile([P, N - PAGE], F32, name="vs_rest", align_bytes=64, offset=4 * PAGE)
+        vs_col = []
+        for u in range(PAGES):
+            vs_g = vs_rest[:, (u - 1) * PAGE : u * PAGE] if u else vs_first[:]
+            nc.vector.tensor_copy(vs_g, vs_win[:].indirect(offs_sb[:, u * PAGE // 16 : (u + 1) * PAGE // 16]))
+            vs_col.append(keep.tile([P, 4], F32, name=f"vs_col{u}"))
+            nc.sync.dma_start(vs_col[u][:], vs_g[0:1, :])
+        vw_g = late.tile([P, PAGES * DV], U32, name="vw_g", align_bytes=64, offset=4 * N)
         nc.vector.tensor_copy(vw_g[:], vw_win[:].bitcast(U32).indirect(voffs_sb[:]))
-        vsc_g = late.tile([P, PAGES * DV], U8, name="vsc_g", align_bytes=64, offset=3648)
-        nc.vector.tensor_copy(vsc_g[:], vsc_win[:].indirect(voffs_sb[:]))
 
         p = [[None] * PAGES for c in range(QT)]
         part = keep.tile([P, QT, PAGES], F32, name="part")

@@ -7,10 +7,20 @@ N, T, D, DV, NQ = 1536, 4096, 1024, 128, 256
 PAGE = 512
 CAP = 2.0
 P = 128
+PLACES = 4
+QUADS = 4
+QUAD = P // QUADS
+ROWS = 4
+STRIPE = 16
 PAGES = N // PAGE
-PASSES = D // 512
+PASSES = D // PAGE
 QT = NQ // P
 POOL_PAGES = T // PAGE
+LAST = PAGES - 1
+KS_ROW0 = P - PASSES * QUADS * ROWS
+PAD = 8
+RUN = 8
+F32_BYTES = 4
 FLOPS = 2 * NQ * N * (D + DV)
 
 F32 = mybir.dt.float32
@@ -26,20 +36,24 @@ ACT = mybir.ActivationFunctionType
 AX = mybir.AxisListType
 
 
+def width(u):
+    return PAGE + (1 if u == LAST else 0)
+
+
 def tile_attend_pkv4q_soft_cap_sink_kernel(
     tc, q_words, q_scales, k_words, k_scales, v_words, v_scales, vs, sink, offs, voffs, out
 ):
     nc = tc.nc
     with ExitStack() as ctx:
         keep = ctx.enter_context(tc.tile_pool(name="keep", bufs=1))
-        ring = ctx.enter_context(tc.tile_pool(name="ring", bufs=3))
+        ring = ctx.enter_context(tc.tile_pool(name="ring", bufs=PAGES))
         late = ctx.enter_context(tc.tile_pool(name="late", bufs=1))
         mid = ctx.enter_context(tc.tile_pool(name="mid", bufs=1))
-        ps_w = ctx.enter_context(tc.psum_pool(name="ps_w", bufs=6))
+        ps_w = ctx.enter_context(tc.psum_pool(name="ps_w", bufs=QT * PAGES))
         ps_o = ctx.enter_context(tc.psum_pool(name="ps_o", bufs=1))
 
-        offs_sb = keep.tile([P, N // 16], U16, name="offs_sb")
-        voffs_sb = keep.tile([P, PAGES * DV // 16], U16, name="voffs_sb")
+        offs_sb = keep.tile([P, N // STRIPE], U16, name="offs_sb")
+        voffs_sb = keep.tile([P, PAGES * DV // STRIPE], U16, name="voffs_sb")
         ks_win = keep.tile([P, T], U8, name="ks_win", tag="ks_win", align_bytes=64)
         kw_win = keep.tile([P, T], I32, name="kw_win", align_bytes=64)
         vsc_win = keep.tile([P, POOL_PAGES * DV], U8, name="vsc_win", align_bytes=64)
@@ -47,16 +61,21 @@ def tile_attend_pkv4q_soft_cap_sink_kernel(
         k_planes = keep.tile([P, PASSES * N], U8, name="k_planes", align_bytes=64)
         sink_sb = keep.tile([P, QT], F32, name="sink_sb")
         ident = keep.tile([P, P], F32, name="ident", align_bytes=64)
-        warm = keep.tile([P, 1], F32, name="warm")
+
+        def page_list(u):
+            return offs_sb[:, u * PAGE // STRIPE : (u + 1) * PAGE // STRIPE]
+
+        def plane_rows(plane, quad, groups):
+            rows = plane[QUAD * quad : QUAD * quad + ROWS, :].bitcast(I32)
+            return rows.rearrange("f (g x) -> f g x", g=groups)
 
         nc.gpsimd.memset(vsc_win[:].bitcast(I32), 0)
-        nc.gpsimd.memset(warm[:], 0.0)
         make_identity(nc, ident[:])
-        nc.vector.memset(ks_win[0:96, :].bitcast(I32), 0)
+        nc.vector.memset(ks_win[0:KS_ROW0, :].bitcast(I32), 0)
         nc.vector.memset(k_planes[:].bitcast(I32), 0)
 
+        nc.sync.dma_start(ks_win[KS_ROW0:P, :].bitcast(I32), k_scales.rearrange("o f t -> f o t").bitcast(I32))
         nc.sync.dma_start(offs_sb[:], offs)
-        nc.sync.dma_start(ks_win[96:P, :].bitcast(I32), k_scales.rearrange("o f t -> f o t").bitcast(I32))
         nc.sync.dma_start(voffs_sb[:], voffs)
         nc.sync.dma_start(kw_win[:], k_words[0].rearrange("g t b -> g (t b)").bitcast(I32))
         nc.sync.dma_start(
@@ -65,80 +84,82 @@ def tile_attend_pkv4q_soft_cap_sink_kernel(
         )
         with nc.allow_non_contiguous_dma(reason="one logit a partition"):
             nc.sync.dma_start(sink_sb[:], sink[0].rearrange("(c p) o -> p (c o)", p=P))
-        for quad in range(4):
+        for quad in range(QUADS):
             nc.scalar.dma_start(
-                vsc_win[32 * quad : 32 * quad + 4, :].bitcast(I32).rearrange("f (u e) -> f u e", u=POOL_PAGES),
-                v_scales[:, 4 * quad : 4 * quad + 4, :].rearrange("u f e -> f u e").bitcast(I32),
+                plane_rows(vsc_win, quad, POOL_PAGES),
+                v_scales[:, ROWS * quad : ROWS * (quad + 1), :].rearrange("u f e -> f u e").bitcast(I32),
             )
-        nc.scalar.activation(warm[:], warm[:], ACT.Exp)
 
-        ks_g = mid.tile([P, N], U8, name="ks_g", align_bytes=64, offset=4 * T - N // 2)
+        border = F32_BYTES * T
+        ks_g = mid.tile([P, N], U8, name="ks_g", align_bytes=64, offset=border - N // 2)
         nc.vector.tensor_copy(ks_g[:], ks_win[:].indirect(offs_sb[:]))
-        for quad in range(4):
+        for quad in range(QUADS):
+            first = KS_ROW0 + PASSES * ROWS * quad
             nc.scalar.dma_start(
-                k_planes[32 * quad : 32 * quad + 4, :].bitcast(I32).rearrange("f (o n) -> f o n", o=PASSES),
-                ks_g[96 + 8 * quad : 96 + 8 * quad + 8, :].bitcast(I32),
+                plane_rows(k_planes, quad, PASSES),
+                ks_g[first : first + PASSES * ROWS, :].bitcast(I32),
             )
         qs = keep.tile([P, PASSES * NQ], U8, name="qs", tag="ks_win", align_bytes=64)
         nc.vector.memset(qs[:].bitcast(I32), 0)
-        for quad in range(4):
+        for quad in range(QUADS):
             nc.sync.dma_start(
-                qs[32 * quad : 32 * quad + 4, :].bitcast(I32).rearrange("f (o q) -> f o q", o=PASSES),
-                q_scales[0, :, 4 * quad : 4 * quad + 4, :].rearrange("o f q -> f o q").bitcast(I32),
+                plane_rows(qs, quad, PASSES),
+                q_scales[0, :, ROWS * quad : ROWS * (quad + 1), :].rearrange("o f q -> f o q").bitcast(I32),
             )
         vsc_g = keep.tile([P, PAGES * DV], U8, name="vsc_g", align_bytes=64)
         nc.vector.tensor_copy(vsc_g[:], vsc_win[:].indirect(voffs_sb[:]))
 
         vs_win = mid.tile([P, T], F32, name="vs_win", align_bytes=64, offset=0)
         nc.sync.dma_start(vs_win[:], vs)
-        vw_win = mid.tile([P, POOL_PAGES * DV], I32, name="vw_win", align_bytes=64, offset=4 * T)
+        vw_win = mid.tile([P, POOL_PAGES * DV], I32, name="vw_win", align_bytes=64, offset=border)
         nc.sync.dma_start(
             vw_win[:].rearrange("g (u e) -> g u e", u=POOL_PAGES),
             v_words.rearrange("u g e r -> g u (e r)").bitcast(I32),
         )
 
-        def width(u):
-            return PAGE + (1 if u == PAGES - 1 else 0)
-
+        late_border = F32_BYTES * N
         th = [
-            [keep.tile([P, PAGE + 8], F32, name=f"th{c}{u}", align_bytes=64) if (c, u) != (QT - 1, PAGES - 1) else None for u in range(PAGES)]
+            [
+                keep.tile([P, PAGE + PAD], F32, name=f"th{c}{u}", align_bytes=64)
+                for u in range(PAGES)
+                if (c, u) != (QT - 1, LAST)
+            ]
             for c in range(QT)
         ]
-        th[QT - 1][PAGES - 1] = late.tile([P, PAGE + 8], F32, name="th_last", align_bytes=64, offset=4 * N - 64)
+        th[QT - 1].append(late.tile([P, PAGE + PAD], F32, name="th_last", align_bytes=64, offset=late_border - 64))
         for c in range(QT):
-            nc.scalar.activation(th[c][PAGES - 1][:, PAGE : PAGE + 1], sink_sb[:, c : c + 1], ACT.Copy, scale=1.0 / CAP)
+            nc.scalar.activation(th[c][LAST][:, PAGE : PAGE + 1], sink_sb[:, c : c + 1], ACT.Copy, scale=1.0 / CAP)
 
         for u in range(PAGES):
             kg = ring.tile([P, PAGE], U32, name="kg", align_bytes=64, bufs=2)
-            nc.vector.tensor_copy(kg[:], kw_win[:].bitcast(U32).indirect(offs_sb[:, u * PAGE // 16 : (u + 1) * PAGE // 16]))
+            nc.vector.tensor_copy(kg[:], kw_win[:].bitcast(U32).indirect(page_list(u)))
             kp = ring.tile([P, PASSES * PAGE], U16, name="kp", align_bytes=64)
             nc.vector.tensor_copy(
-                kp[:].rearrange("p (o c i) -> p c o i", o=PASSES, i=8),
-                kg[:].bitcast(U16).rearrange("p (c i o) -> p c o i", o=PASSES, i=8),
+                kp[:].rearrange("p (o n i) -> p n o i", o=PASSES, i=RUN),
+                kg[:].bitcast(U16).rearrange("p (n i o) -> p n o i", o=PASSES, i=RUN),
             )
             for c in range(QT):
-                s = ps_w.tile([P, PAGE], F32, name="s", tag="bank")
+                scores = ps_w.tile([P, PAGE], F32, name="scores", tag="bank")
                 for o in range(PASSES):
-                    qc = slice(o * NQ + c * P, o * NQ + (c + 1) * P)
+                    q_cols = slice(o * NQ + c * P, o * NQ + (c + 1) * P)
                     nc.tensor.matmul_mx(
-                        out=s[:],
-                        lhsT=qw[:, qc].bitcast(FP8X4),
-                        lhsT_scale=qs[:, qc],
+                        out=scores[:],
+                        lhsT=qw[:, q_cols].bitcast(FP8X4),
+                        lhsT_scale=qs[:, q_cols],
                         rhs=kp[:, o * PAGE : (o + 1) * PAGE].bitcast(FP4X4),
                         rhs_scale=k_planes[:, o * N + u * PAGE : o * N + (u + 1) * PAGE],
                         start=(o == 0),
                         stop=(o == PASSES - 1),
                     )
                 nc.scalar.activation(
-                    th[c][u][:, 0:PAGE].rearrange("p (t s) -> p t s", t=4),
-                    s[:].rearrange("p (s t) -> p t s", t=4),
+                    th[c][u][:, 0:PAGE].rearrange("p (t s) -> p t s", t=PLACES),
+                    scores[:].rearrange("p (s t) -> p t s", t=PLACES),
                     ACT.Tanh,
                     scale=1.0 / CAP,
                 )
 
-        neg_c = [keep.tile([P, N + 8], F32, name=f"neg_c{c}", align_bytes=64) for c in range(QT)]
+        neg_c = [keep.tile([P, N + PAD], F32, name=f"neg_c{c}", align_bytes=64) for c in range(QT)]
         neg_m = [keep.tile([P, PAGES], F32, name=f"neg_m{c}") for c in range(QT)]
-
         for c in range(QT):
             for u in range(PAGES):
                 nc.vector.tensor_scalar(
@@ -152,26 +173,28 @@ def tile_attend_pkv4q_soft_cap_sink_kernel(
                 )
 
         vs_first = keep.tile([P, PAGE], F32, name="vs_first", align_bytes=64)
-        vs_rest = late.tile([P, N - PAGE], F32, name="vs_rest", align_bytes=64, offset=4 * PAGE)
+        vs_rest = late.tile([P, N - PAGE], F32, name="vs_rest", align_bytes=64, offset=F32_BYTES * PAGE)
         vs_col = []
         for u in range(PAGES):
             vs_g = vs_rest[:, (u - 1) * PAGE : u * PAGE] if u else vs_first[:]
-            nc.vector.tensor_copy(vs_g, vs_win[:].indirect(offs_sb[:, u * PAGE // 16 : (u + 1) * PAGE // 16]))
-            vs_col.append(keep.tile([P, 4], F32, name=f"vs_col{u}"))
+            nc.vector.tensor_copy(vs_g, vs_win[:].indirect(page_list(u)))
+            vs_col.append(keep.tile([P, PLACES], F32, name=f"vs_col{u}"))
             nc.sync.dma_start(vs_col[u][:], vs_g[0:1, :])
-        vw_g = late.tile([P, PAGES * DV], U32, name="vw_g", align_bytes=64, offset=4 * N)
+        vw_g = late.tile([P, PAGES * DV], U32, name="vw_g", align_bytes=64, offset=late_border)
         nc.vector.tensor_copy(vw_g[:], vw_win[:].bitcast(U32).indirect(voffs_sb[:]))
 
-        p = [[None] * PAGES for c in range(QT)]
+        prob = [[] for c in range(QT)]
         part = keep.tile([P, QT, PAGES], F32, name="part")
         for c in range(QT):
             for u in range(PAGES):
-                p[c][u] = keep.tile([P, PAGE + 8], F32, name=f"p{c}{u}", tag=f"p{c}{u}", align_bytes=64)
+                prob[c].append(
+                    keep.tile([P, PAGE + PAD], F32, name=f"prob{c}{u}", tag=f"prob{c}{u}", align_bytes=64)
+                )
                 nc.scalar.activation(
-                    p[c][u][:, 0 : width(u)],
+                    prob[c][u][:, 0 : width(u)],
                     neg_c[c][:, u * PAGE : u * PAGE + width(u)],
                     ACT.Exp,
-                    bias=neg_m[c][:, PAGES - 1 : PAGES],
+                    bias=neg_m[c][:, LAST:PAGES],
                     scale=-1.0,
                     accum_out=part[:, c, u : u + 1],
                 )
@@ -183,35 +206,37 @@ def tile_attend_pkv4q_soft_cap_sink_kernel(
         w = [keep.tile([P, N], BF16, name=f"w{c}", align_bytes=64) for c in range(QT)]
         for c in range(QT):
             for u in range(PAGES):
-                pt = ps_w.tile([P, PAGE], F32, name="pt", tag="bank")
-                for t in range(4):
-                    nc.tensor.transpose(pt[:, t * P : (t + 1) * P], p[c][u][:, t * P : (t + 1) * P], ident[:])
+                turned = ps_w.tile([P, PAGE], F32, name="turned", tag="bank")
+                for t in range(PLACES):
+                    quarter = slice(t * P, (t + 1) * P)
+                    nc.tensor.transpose(turned[:, quarter], prob[c][u][:, quarter], ident[:])
                 w_page = w[c][:, u * PAGE : (u + 1) * PAGE]
                 if c == 0:
                     nc.vector.tensor_tensor(
-                        w_page.rearrange("p (q t) -> p q t", t=4),
-                        pt[:].rearrange("p (t q) -> p q t", t=4),
-                        vs_col[u][:].unsqueeze(1).to_broadcast([P, P, 4]),
+                        w_page.rearrange("p (q t) -> p q t", t=PLACES),
+                        turned[:].rearrange("p (t q) -> p q t", t=PLACES),
+                        vs_col[u][:].unsqueeze(1).to_broadcast([P, P, PLACES]),
                         ALU.mult,
                     )
                 else:
-                    flat = ring.tile([P, PAGE], BF16, name="flat", align_bytes=64)
-                    for t in range(4):
+                    pairs = ring.tile([P, PAGE], BF16, name="pairs", align_bytes=64)
+                    for t in range(PLACES):
                         nc.scalar.activation(
-                            flat[:, t * P : (t + 1) * P],
-                            pt[:, t * P : (t + 1) * P],
+                            pairs[:].rearrange("p (h q e) -> p h q e", h=2, e=2)[:, t // 2, :, t % 2],
+                            turned[:, t * P : (t + 1) * P],
                             ACT.Copy,
                             scale=vs_col[u][:, t : t + 1],
                         )
                     nc.vector.tensor_copy(
-                        w_page.rearrange("p (g i t) -> p g t i", i=4, t=4),
-                        flat[:].rearrange("p (t g i) -> p g t i", i=4, t=4),
+                        w_page.bitcast(I32).rearrange("p (q h) -> p q h", h=2),
+                        pairs[:].bitcast(I32).rearrange("p (h q) -> p q h", h=2),
                     )
 
         for c in range(QT):
             wq = keep.tile([P, PAGES * P], U32, name=f"wq{c}", align_bytes=64)
-            ws = keep.tile([P, PAGES * P], U8, name=f"ws{c}", tag="p12" if c == 0 else "ws1", align_bytes=64)
-            for lo, hi in ((0, 2), (2, 3)):
+            ws_tag = f"prob{QT - 1}{LAST}" if c == 0 else f"ws{c}"
+            ws = keep.tile([P, PAGES * P], U8, name=f"ws{c}", tag=ws_tag, align_bytes=64)
+            for lo, hi in ((0, LAST), (LAST, PAGES)):
                 nc.vector.quantize_mx(
                     out=wq[:, lo * P : hi * P].bitcast(FP8X4),
                     scales=ws[:, lo * P : hi * P],
@@ -226,7 +251,7 @@ def tile_attend_pkv4q_soft_cap_sink_kernel(
                     rhs=vw_g[:, u * DV : (u + 1) * DV].bitcast(FP8X4),
                     rhs_scale=vsc_g[:, u * DV : (u + 1) * DV],
                     start=(u == 0),
-                    stop=(u == PAGES - 1),
+                    stop=(u == LAST),
                 )
             y = keep.tile([P, DV], F32, name=f"y{c}", align_bytes=64)
             nc.scalar.activation(y[:], acc[:], ACT.Copy, scale=inv[:, c : c + 1])

@@ -21,6 +21,10 @@ KS_ROW0 = P - PASSES * QUADS * ROWS
 PAD = 8
 RUN = 8
 F32_BYTES = 4
+STAGE = N + NQ
+VW_BYTES = F32_BYTES * POOL_PAGES * DV
+VS_ROW = P - 1
+ON_SCALAR = (QT - 1, LAST - 1)
 FLOPS = 2 * NQ * N * (D + DV)
 
 F32 = mybir.dt.float32
@@ -49,16 +53,16 @@ def tile_attend_pkv4q_soft_cap_sink_kernel(
         ring = ctx.enter_context(tc.tile_pool(name="ring", bufs=PAGES))
         late = ctx.enter_context(tc.tile_pool(name="late", bufs=1))
         mid = ctx.enter_context(tc.tile_pool(name="mid", bufs=1))
-        ps_w = ctx.enter_context(tc.psum_pool(name="ps_w", bufs=QT * PAGES))
-        ps_o = ctx.enter_context(tc.psum_pool(name="ps_o", bufs=1))
+        ps_w = ctx.enter_context(tc.psum_pool(name="ps_w", bufs=1))
 
         offs_sb = keep.tile([P, N // STRIPE], U16, name="offs_sb")
         voffs_sb = keep.tile([P, PAGES * DV // STRIPE], U16, name="voffs_sb")
-        ks_win = keep.tile([P, T], U8, name="ks_win", tag="ks_win", align_bytes=64)
+        ks_win = keep.tile([P, T], U8, name="ks_win", align_bytes=64)
+        vs_win = keep.tile([P, T], F32, name="vs_win", align_bytes=64)
         kw_win = keep.tile([P, T], I32, name="kw_win", align_bytes=64)
-        vsc_win = keep.tile([P, POOL_PAGES * DV], U8, name="vsc_win", align_bytes=64)
         qw = keep.tile([P, PASSES * NQ], I32, name="qw", align_bytes=64)
-        k_planes = keep.tile([P, PASSES * N], U8, name="k_planes", align_bytes=64)
+        planes = keep.tile([P, PASSES * STAGE], U8, name="planes", align_bytes=64)
+        stage = mid.tile([P, STAGE], U8, name="stage", align_bytes=64, offset=VW_BYTES - STAGE // 2)
         sink_sb = keep.tile([P, QT], F32, name="sink_sb")
         ident = keep.tile([P, P], F32, name="ident", align_bytes=64)
 
@@ -69,55 +73,57 @@ def tile_attend_pkv4q_soft_cap_sink_kernel(
             rows = plane[QUAD * quad : QUAD * quad + ROWS, :].bitcast(I32)
             return rows.rearrange("f (g x) -> f g x", g=groups)
 
-        nc.gpsimd.memset(vsc_win[:].bitcast(I32), 0)
-        make_identity(nc, ident[:])
         nc.vector.memset(ks_win[0:KS_ROW0, :].bitcast(I32), 0)
-        nc.vector.memset(k_planes[:].bitcast(I32), 0)
+        nc.vector.memset(planes[:].bitcast(I32), 0)
+        nc.vector.memset(vs_win[0:VS_ROW, :], 0.0)
 
-        nc.sync.dma_start(ks_win[KS_ROW0:P, :].bitcast(I32), k_scales.rearrange("o f t -> f o t").bitcast(I32))
         nc.sync.dma_start(offs_sb[:], offs)
-        nc.sync.dma_start(voffs_sb[:], voffs)
+        nc.sync.dma_start(ks_win[KS_ROW0:P, :].bitcast(I32), k_scales.rearrange("o f t -> f o t").bitcast(I32))
+        nc.sync.dma_start(
+            stage[KS_ROW0:P, N:STAGE].bitcast(I32), q_scales[0].rearrange("o f q -> f o q").bitcast(I32)
+        )
+        nc.sync.dma_start(vs_win[VS_ROW:P, :], vs[0:1, :])
         nc.sync.dma_start(kw_win[:], k_words[0].rearrange("g t b -> g (t b)").bitcast(I32))
         nc.sync.dma_start(
             qw[:].rearrange("g (o q) -> g o q", o=PASSES),
             q_words[0].rearrange("o g q r -> g o (q r)").bitcast(I32),
         )
+        nc.sync.dma_start(voffs_sb[:], voffs)
         with nc.allow_non_contiguous_dma(reason="one logit a partition"):
             nc.sync.dma_start(sink_sb[:], sink[0].rearrange("(c p) o -> p (c o)", p=P))
-        for quad in range(QUADS):
-            nc.scalar.dma_start(
-                plane_rows(vsc_win, quad, POOL_PAGES),
-                v_scales[:, ROWS * quad : ROWS * (quad + 1), :].rearrange("u f e -> f u e").bitcast(I32),
-            )
+        make_identity(nc, ident[:])
 
-        border = F32_BYTES * T
-        ks_g = mid.tile([P, N], U8, name="ks_g", align_bytes=64, offset=border - N // 2)
+        ks_g = keep.tile([P, N], U8, name="ks_g", align_bytes=64)
         nc.vector.tensor_copy(ks_g[:], ks_win[:].indirect(offs_sb[:]))
+        nc.vector.tensor_copy(stage[KS_ROW0:P, 0:N].bitcast(I32), ks_g[KS_ROW0:P, :].bitcast(I32))
         for quad in range(QUADS):
             first = KS_ROW0 + PASSES * ROWS * quad
             nc.scalar.dma_start(
-                plane_rows(k_planes, quad, PASSES),
-                ks_g[first : first + PASSES * ROWS, :].bitcast(I32),
+                plane_rows(planes, quad, PASSES),
+                stage[first : first + PASSES * ROWS, :].bitcast(I32),
             )
-        qs = keep.tile([P, PASSES * NQ], U8, name="qs", tag="ks_win", align_bytes=64)
-        nc.vector.memset(qs[:].bitcast(I32), 0)
-        for quad in range(QUADS):
-            nc.sync.dma_start(
-                plane_rows(qs, quad, PASSES),
-                q_scales[0, :, ROWS * quad : ROWS * (quad + 1), :].rearrange("o f q -> f o q").bitcast(I32),
-            )
-        vsc_g = keep.tile([P, PAGES * DV], U8, name="vsc_g", align_bytes=64)
-        nc.vector.tensor_copy(vsc_g[:], vsc_win[:].indirect(voffs_sb[:]))
 
-        vs_win = mid.tile([P, T], F32, name="vs_win", align_bytes=64, offset=0)
-        nc.sync.dma_start(vs_win[:], vs)
-        vw_win = mid.tile([P, POOL_PAGES * DV], I32, name="vw_win", align_bytes=64, offset=border)
+        vs_g = keep.tile([P, N], F32, name="vs_g", align_bytes=64)
+        nc.vector.tensor_copy(vs_g[:], vs_win[:].indirect(offs_sb[:]))
+        vs_col = []
+        for u in range(PAGES):
+            vs_col.append(keep.tile([P, PLACES], F32, name=f"vs_col{u}"))
+            nc.sync.dma_start(vs_col[u][:], vs_g[VS_ROW:P, u * PAGE : (u + 1) * PAGE])
+
+        vw_win = mid.tile([P, POOL_PAGES * DV], I32, name="vw_win", align_bytes=64, offset=0)
         nc.sync.dma_start(
             vw_win[:].rearrange("g (u e) -> g u e", u=POOL_PAGES),
             v_words.rearrange("u g e r -> g u (e r)").bitcast(I32),
         )
 
-        late_border = F32_BYTES * N
+        vsc_win = mid.tile([P, POOL_PAGES * DV], U8, name="vsc_win", align_bytes=64, offset=VW_BYTES)
+        nc.gpsimd.memset(vsc_win[:].bitcast(I32), 0)
+        for quad in range(QUADS):
+            nc.sync.dma_start(
+                plane_rows(vsc_win, quad, POOL_PAGES),
+                v_scales[:, ROWS * quad : ROWS * (quad + 1), :].rearrange("u f e -> f u e").bitcast(I32),
+            )
+
         th = [
             [
                 keep.tile([P, PAGE + PAD], F32, name=f"th{c}{u}", align_bytes=64)
@@ -126,9 +132,11 @@ def tile_attend_pkv4q_soft_cap_sink_kernel(
             ]
             for c in range(QT)
         ]
-        th[QT - 1].append(late.tile([P, PAGE + PAD], F32, name="th_last", align_bytes=64, offset=late_border - 64))
+        th[QT - 1].append(late.tile([P, PAGE + PAD], F32, name="th_last", align_bytes=64, offset=0))
         for c in range(QT):
-            nc.scalar.activation(th[c][LAST][:, PAGE : PAGE + 1], sink_sb[:, c : c + 1], ACT.Copy, scale=1.0 / CAP)
+            nc.gpsimd.tensor_scalar(
+                th[c][LAST][:, PAGE : PAGE + 1], sink_sb[:, c : c + 1], 1.0 / CAP, 0.0, ALU.mult, ALU.add
+            )
 
         for u in range(PAGES):
             kg = ring.tile([P, PAGE], U32, name="kg", align_bytes=64, bufs=2)
@@ -139,15 +147,15 @@ def tile_attend_pkv4q_soft_cap_sink_kernel(
                 kg[:].bitcast(U16).rearrange("p (n i o) -> p n o i", o=PASSES, i=RUN),
             )
             for c in range(QT):
-                scores = ps_w.tile([P, PAGE], F32, name="scores", tag="bank")
+                scores = ps_w.tile([P, PAGE], F32, name="scores", tag=f"bank{c}{u}")
                 for o in range(PASSES):
                     q_cols = slice(o * NQ + c * P, o * NQ + (c + 1) * P)
                     nc.tensor.matmul_mx(
                         out=scores[:],
                         lhsT=qw[:, q_cols].bitcast(FP8X4),
-                        lhsT_scale=qs[:, q_cols],
+                        lhsT_scale=planes[:, o * STAGE + N + c * P : o * STAGE + N + (c + 1) * P],
                         rhs=kp[:, o * PAGE : (o + 1) * PAGE].bitcast(FP4X4),
-                        rhs_scale=k_planes[:, o * N + u * PAGE : o * N + (u + 1) * PAGE],
+                        rhs_scale=planes[:, o * STAGE + u * PAGE : o * STAGE + (u + 1) * PAGE],
                         start=(o == 0),
                         stop=(o == PASSES - 1),
                     )
@@ -172,16 +180,10 @@ def tile_attend_pkv4q_soft_cap_sink_kernel(
                     accum_out=neg_m[c][:, u : u + 1],
                 )
 
-        vs_first = keep.tile([P, PAGE], F32, name="vs_first", align_bytes=64)
-        vs_rest = late.tile([P, N - PAGE], F32, name="vs_rest", align_bytes=64, offset=F32_BYTES * PAGE)
-        vs_col = []
-        for u in range(PAGES):
-            vs_g = vs_rest[:, (u - 1) * PAGE : u * PAGE] if u else vs_first[:]
-            nc.vector.tensor_copy(vs_g, vs_win[:].indirect(page_list(u)))
-            vs_col.append(keep.tile([P, PLACES], F32, name=f"vs_col{u}"))
-            nc.sync.dma_start(vs_col[u][:], vs_g[0:1, :])
-        vw_g = late.tile([P, PAGES * DV], U32, name="vw_g", align_bytes=64, offset=late_border)
+        vw_g = late.tile([P, PAGES * DV], U32, name="vw_g", align_bytes=64, offset=0)
         nc.vector.tensor_copy(vw_g[:], vw_win[:].bitcast(U32).indirect(voffs_sb[:]))
+        vsc_g = late.tile([P, PAGES * DV], U8, name="vsc_g", align_bytes=64, offset=F32_BYTES * PAGES * DV)
+        nc.vector.tensor_copy(vsc_g[:], vsc_win[:].indirect(voffs_sb[:]))
 
         prob = [[] for c in range(QT)]
         part = keep.tile([P, QT, PAGES], F32, name="part")
@@ -206,12 +208,12 @@ def tile_attend_pkv4q_soft_cap_sink_kernel(
         w = [keep.tile([P, N], BF16, name=f"w{c}", align_bytes=64) for c in range(QT)]
         for c in range(QT):
             for u in range(PAGES):
-                turned = ps_w.tile([P, PAGE], F32, name="turned", tag="bank")
+                turned = ps_w.tile([P, PAGE], F32, name="turned", tag=f"bank{c}{u}")
                 for t in range(PLACES):
                     quarter = slice(t * P, (t + 1) * P)
                     nc.tensor.transpose(turned[:, quarter], prob[c][u][:, quarter], ident[:])
                 w_page = w[c][:, u * PAGE : (u + 1) * PAGE]
-                if c == 0:
+                if (c, u) != ON_SCALAR:
                     nc.vector.tensor_tensor(
                         w_page.rearrange("p (q t) -> p q t", t=PLACES),
                         turned[:].rearrange("p (t q) -> p q t", t=PLACES),
@@ -234,15 +236,14 @@ def tile_attend_pkv4q_soft_cap_sink_kernel(
 
         for c in range(QT):
             wq = keep.tile([P, PAGES * P], U32, name=f"wq{c}", align_bytes=64)
-            ws_tag = f"prob{QT - 1}{LAST}" if c == 0 else f"ws{c}"
-            ws = keep.tile([P, PAGES * P], U8, name=f"ws{c}", tag=ws_tag, align_bytes=64)
-            for lo, hi in ((0, LAST), (LAST, PAGES)):
+            ws = keep.tile([P, PAGES * P], U8, name=f"ws{c}", align_bytes=64)
+            for lo, hi in ((0, LAST), (LAST, PAGES)) if c == 0 else ((0, 1), (1, PAGES)):
                 nc.vector.quantize_mx(
                     out=wq[:, lo * P : hi * P].bitcast(FP8X4),
                     scales=ws[:, lo * P : hi * P],
                     in_=w[c][:, lo * PAGE : hi * PAGE],
                 )
-            acc = ps_o.tile([P, DV], F32, name=f"acc{c}")
+            acc = ps_w.tile([P, DV], F32, name=f"acc{c}", tag=f"bank{QT - 1}{LAST - 1 - c}")
             for u in range(PAGES):
                 nc.tensor.matmul_mx(
                     out=acc[:],

@@ -21,6 +21,7 @@ KS_ROW0 = P - PASSES * QUADS * ROWS
 PAD = 8
 RUN = 8
 F32_BYTES = 4
+SCORE_ORDER = ((0, 0), (1, 0), (0, 1), (0, 2), (1, 1), (1, 2))
 STAGE = N + NQ
 VW_BYTES = F32_BYTES * POOL_PAGES * DV
 VS_ROW = P - 1
@@ -57,11 +58,10 @@ def tile_attend_pkv4q_soft_cap_sink_kernel(
 
         offs_sb = keep.tile([P, N // STRIPE], U16, name="offs_sb")
         voffs_sb = keep.tile([P, PAGES * DV // STRIPE], U16, name="voffs_sb")
-        ks_win = keep.tile([P, T], U8, name="ks_win", align_bytes=64)
+        ks_win = keep.tile([P, T], U8, name="ks_win", tag="ks_win", align_bytes=64)
         vs_win = keep.tile([P, T], F32, name="vs_win", align_bytes=64)
         kw_win = keep.tile([P, T], I32, name="kw_win", align_bytes=64)
         qw = keep.tile([P, PASSES * NQ], I32, name="qw", align_bytes=64)
-        planes = keep.tile([P, PASSES * STAGE], U8, name="planes", align_bytes=64)
         stage = mid.tile([P, STAGE], U8, name="stage", align_bytes=64, offset=VW_BYTES - STAGE // 2)
         sink_sb = keep.tile([P, QT], F32, name="sink_sb")
         ident = keep.tile([P, P], F32, name="ident", align_bytes=64)
@@ -74,15 +74,14 @@ def tile_attend_pkv4q_soft_cap_sink_kernel(
             return rows.rearrange("f (g x) -> f g x", g=groups)
 
         nc.vector.memset(ks_win[0:KS_ROW0, :].bitcast(I32), 0)
-        nc.vector.memset(planes[:].bitcast(I32), 0)
         nc.vector.memset(vs_win[0:VS_ROW, :], 0.0)
 
         nc.sync.dma_start(offs_sb[:], offs)
         nc.sync.dma_start(ks_win[KS_ROW0:P, :].bitcast(I32), k_scales.rearrange("o f t -> f o t").bitcast(I32))
-        nc.sync.dma_start(
+        nc.scalar.dma_start(
             stage[KS_ROW0:P, N:STAGE].bitcast(I32), q_scales[0].rearrange("o f q -> f o q").bitcast(I32)
         )
-        nc.sync.dma_start(vs_win[VS_ROW:P, :], vs[0:1, :])
+        nc.scalar.dma_start(vs_win[VS_ROW:P, :], vs[0:1, :])
         nc.sync.dma_start(kw_win[:], k_words[0].rearrange("g t b -> g (t b)").bitcast(I32))
         nc.sync.dma_start(
             qw[:].rearrange("g (o q) -> g o q", o=PASSES),
@@ -90,12 +89,13 @@ def tile_attend_pkv4q_soft_cap_sink_kernel(
         )
         nc.sync.dma_start(voffs_sb[:], voffs)
         with nc.allow_non_contiguous_dma(reason="one logit a partition"):
-            nc.sync.dma_start(sink_sb[:], sink[0].rearrange("(c p) o -> p (c o)", p=P))
+            nc.scalar.dma_start(sink_sb[:], sink[0].rearrange("(c p) o -> p (c o)", p=P))
         make_identity(nc, ident[:])
 
         ks_g = keep.tile([P, N], U8, name="ks_g", align_bytes=64)
         nc.vector.tensor_copy(ks_g[:], ks_win[:].indirect(offs_sb[:]))
         nc.vector.tensor_copy(stage[KS_ROW0:P, 0:N].bitcast(I32), ks_g[KS_ROW0:P, :].bitcast(I32))
+        planes = keep.tile([P, PASSES * STAGE], U8, name="planes", tag="ks_win", align_bytes=64)
         for quad in range(QUADS):
             first = KS_ROW0 + PASSES * ROWS * quad
             nc.scalar.dma_start(
@@ -138,47 +138,55 @@ def tile_attend_pkv4q_soft_cap_sink_kernel(
                 th[c][LAST][:, PAGE : PAGE + 1], sink_sb[:, c : c + 1], 1.0 / CAP, 0.0, ALU.mult, ALU.add
             )
 
+        kp = []
         for u in range(PAGES):
             kg = ring.tile([P, PAGE], U32, name="kg", align_bytes=64, bufs=2)
             nc.vector.tensor_copy(kg[:], kw_win[:].bitcast(U32).indirect(page_list(u)))
-            kp = ring.tile([P, PASSES * PAGE], U16, name="kp", align_bytes=64)
-            nc.vector.tensor_copy(
-                kp[:].rearrange("p (o n i) -> p n o i", o=PASSES, i=RUN),
-                kg[:].bitcast(U16).rearrange("p (n i o) -> p n o i", o=PASSES, i=RUN),
-            )
-            for c in range(QT):
-                scores = ps_w.tile([P, PAGE], F32, name="scores", tag=f"bank{c}{u}")
+            kp.append(ring.tile([P, PASSES * PAGE], U16, name="kp", align_bytes=64))
+            if u == 0:
                 for o in range(PASSES):
-                    q_cols = slice(o * NQ + c * P, o * NQ + (c + 1) * P)
-                    nc.tensor.matmul_mx(
-                        out=scores[:],
-                        lhsT=qw[:, q_cols].bitcast(FP8X4),
-                        lhsT_scale=planes[:, o * STAGE + N + c * P : o * STAGE + N + (c + 1) * P],
-                        rhs=kp[:, o * PAGE : (o + 1) * PAGE].bitcast(FP4X4),
-                        rhs_scale=planes[:, o * STAGE + u * PAGE : o * STAGE + (u + 1) * PAGE],
-                        start=(o == 0),
-                        stop=(o == PASSES - 1),
+                    nc.vector.tensor_copy(
+                        kp[u][:, o * PAGE : (o + 1) * PAGE],
+                        kg[:].bitcast(U16).rearrange("p (n o) -> p n o", o=PASSES)[:, :, o],
                     )
-                nc.scalar.activation(
-                    th[c][u][:, 0:PAGE].rearrange("p (t s) -> p t s", t=PLACES),
-                    scores[:].rearrange("p (s t) -> p t s", t=PLACES),
-                    ACT.Tanh,
-                    scale=1.0 / CAP,
+            else:
+                nc.vector.tensor_copy(
+                    kp[u][:].rearrange("p (o n i) -> p n o i", o=PASSES, i=RUN),
+                    kg[:].bitcast(U16).rearrange("p (n i o) -> p n o i", o=PASSES, i=RUN),
                 )
+
+        for c, u in SCORE_ORDER:
+            scores = ps_w.tile([P, PAGE], F32, name="scores", tag=f"bank{c}{u}")
+            for o in range(PASSES):
+                q_cols = slice(o * NQ + c * P, o * NQ + (c + 1) * P)
+                nc.tensor.matmul_mx(
+                    out=scores[:],
+                    lhsT=qw[:, q_cols].bitcast(FP8X4),
+                    lhsT_scale=planes[:, o * STAGE + N + c * P : o * STAGE + N + (c + 1) * P],
+                    rhs=kp[u][:, o * PAGE : (o + 1) * PAGE].bitcast(FP4X4),
+                    rhs_scale=planes[:, o * STAGE + u * PAGE : o * STAGE + (u + 1) * PAGE],
+                    start=(o == 0),
+                    stop=(o == PASSES - 1),
+                )
+            nc.scalar.activation(
+                th[c][u][:, 0:PAGE].rearrange("p (t s) -> p s t", t=PLACES),
+                scores[:].rearrange("p (s t) -> p s t", t=PLACES),
+                ACT.Tanh,
+                scale=1.0 / CAP,
+            )
 
         neg_c = [keep.tile([P, N + PAD], F32, name=f"neg_c{c}", align_bytes=64) for c in range(QT)]
         neg_m = [keep.tile([P, PAGES], F32, name=f"neg_m{c}") for c in range(QT)]
-        for c in range(QT):
-            for u in range(PAGES):
-                nc.vector.tensor_scalar(
-                    neg_c[c][:, u * PAGE : u * PAGE + width(u)],
-                    th[c][u][:, 0 : width(u)],
-                    -CAP,
-                    neg_m[c][:, u - 1 : u] if u else None,
-                    ALU.mult,
-                    ALU.min,
-                    accum_out=neg_m[c][:, u : u + 1],
-                )
+        for c, u in SCORE_ORDER:
+            nc.vector.tensor_scalar(
+                neg_c[c][:, u * PAGE : u * PAGE + width(u)],
+                th[c][u][:, 0 : width(u)],
+                -CAP,
+                neg_m[c][:, u - 1 : u] if u else None,
+                ALU.mult,
+                ALU.min,
+                accum_out=neg_m[c][:, u : u + 1],
+            )
 
         vw_g = late.tile([P, PAGES * DV], U32, name="vw_g", align_bytes=64, offset=0)
         nc.vector.tensor_copy(vw_g[:], vw_win[:].bitcast(U32).indirect(voffs_sb[:]))
@@ -186,20 +194,24 @@ def tile_attend_pkv4q_soft_cap_sink_kernel(
         nc.vector.tensor_copy(vsc_g[:], vsc_win[:].indirect(voffs_sb[:]))
 
         prob = [[] for c in range(QT)]
-        part = keep.tile([P, QT, PAGES], F32, name="part")
+        part = keep.tile([P, QT, PAGES + 1], F32, name="part")
         for c in range(QT):
             for u in range(PAGES):
                 prob[c].append(
                     keep.tile([P, PAGE + PAD], F32, name=f"prob{c}{u}", tag=f"prob{c}{u}", align_bytes=64)
                 )
-                nc.scalar.activation(
-                    prob[c][u][:, 0 : width(u)],
-                    neg_c[c][:, u * PAGE : u * PAGE + width(u)],
-                    ACT.Exp,
-                    bias=neg_m[c][:, LAST:PAGES],
-                    scale=-1.0,
-                    accum_out=part[:, c, u : u + 1],
-                )
+                halved = LAST * c
+                cuts = (0, PAGE // 2, width(u)) if u == halved else (0, width(u))
+                col = u + (u > halved)
+                for j in range(len(cuts) - 1):
+                    nc.scalar.activation(
+                        prob[c][u][:, cuts[j] : cuts[j + 1]],
+                        neg_c[c][:, u * PAGE + cuts[j] : u * PAGE + cuts[j + 1]],
+                        ACT.Exp,
+                        bias=neg_m[c][:, LAST:PAGES],
+                        scale=-1.0,
+                        accum_out=part[:, c, col + j : col + j + 1],
+                    )
         total = keep.tile([P, QT], F32, name="total")
         nc.vector.tensor_reduce(total[:], part[:], AX.X, ALU.add)
         inv = keep.tile([P, QT], F32, name="inv")

@@ -21,6 +21,7 @@ KS_ROW0 = P - PASSES * QUADS * ROWS
 PAD = 8
 RUN = 8
 F32_BYTES = 4
+VS_CUT = 7 * T // 8
 SCORE_ORDER = ((0, 0), (1, 0), (0, 1), (0, 2), (1, 1), (1, 2))
 STAGE = N + NQ
 VW_BYTES = F32_BYTES * POOL_PAGES * DV
@@ -74,7 +75,7 @@ def tile_attend_pkv4q_soft_cap_sink_kernel(
             return rows.rearrange("f (g x) -> f g x", g=groups)
 
         nc.vector.memset(ks_win[0:KS_ROW0, :].bitcast(I32), 0)
-        nc.vector.memset(vs_win[0:VS_ROW, :], 0.0)
+        nc.vector.memset(vs_win[0:VS_ROW, 0:VS_CUT], 0.0)
 
         nc.sync.dma_start(offs_sb[:], offs)
         nc.sync.dma_start(ks_win[KS_ROW0:P, :].bitcast(I32), k_scales.rearrange("o f t -> f o t").bitcast(I32))
@@ -96,6 +97,7 @@ def tile_attend_pkv4q_soft_cap_sink_kernel(
         nc.vector.tensor_copy(ks_g[:], ks_win[:].indirect(offs_sb[:]))
         nc.vector.tensor_copy(stage[KS_ROW0:P, 0:N].bitcast(I32), ks_g[KS_ROW0:P, :].bitcast(I32))
         planes = keep.tile([P, PASSES * STAGE], U8, name="planes", tag="ks_win", align_bytes=64)
+        nc.vector.memset(vs_win[0:VS_ROW, VS_CUT:T], 0.0)
         for quad in range(QUADS):
             first = KS_ROW0 + PASSES * ROWS * quad
             nc.scalar.dma_start(
@@ -169,8 +171,8 @@ def tile_attend_pkv4q_soft_cap_sink_kernel(
                     stop=(o == PASSES - 1),
                 )
             nc.scalar.activation(
-                th[c][u][:, 0:PAGE].rearrange("p (t s) -> p s t", t=PLACES),
-                scores[:].rearrange("p (s t) -> p s t", t=PLACES),
+                th[c][u][:, 0:PAGE].rearrange("p (t s) -> p t s", t=PLACES),
+                scores[:].rearrange("p (s t) -> p t s", t=PLACES),
                 ACT.Tanh,
                 scale=1.0 / CAP,
             )

@@ -21,6 +21,7 @@ KS_ROW0 = P - PASSES * QUADS * ROWS
 PAD = 8
 RUN = 8
 F32_BYTES = 4
+WARM_UPS = 2
 VS_CUT = 7 * T // 8
 SCORE_ORDER = ((0, 0), (1, 0), (0, 1), (0, 2), (1, 1), (1, 2))
 STAGE = N + NQ
@@ -142,8 +143,20 @@ def tile_attend_pkv4q_soft_cap_sink_kernel(
 
         kp = []
         for u in range(PAGES):
-            kg = ring.tile([P, PAGE], U32, name="kg", align_bytes=64, bufs=2)
+            kg = ring.tile([P, PAGE], U32, name="kg", align_bytes=64)
             nc.vector.tensor_copy(kg[:], kw_win[:].bitcast(U32).indirect(page_list(u)))
+            if u == 0:
+                warm = ps_w.tile([P, PAGE], F32, name="warm")
+                for j in range(WARM_UPS):
+                    nc.tensor.matmul_mx(
+                        out=warm[:],
+                        lhsT=qw[:, 0:P].bitcast(FP8X4),
+                        lhsT_scale=ks_g[:, 0:P],
+                        rhs=kg[:].bitcast(U16)[:, 0:PAGE].bitcast(FP4X4),
+                        rhs_scale=ks_g[:, 0:PAGE],
+                        start=True,
+                        stop=True,
+                    )
             kp.append(ring.tile([P, PASSES * PAGE], U16, name="kp", align_bytes=64))
             if u == 0:
                 for o in range(PASSES):

@@ -17,7 +17,7 @@ PASSES = D // PAGE
 QT = NQ // P
 POOL_PAGES = T // PAGE
 LAST = PAGES - 1
-KS_ROW0 = P - PASSES * QUADS * ROWS
+KS_ROW0, KS_ROW1 = QUAD, 2 * QUAD
 PAD = 8
 RUN = 8
 F32_BYTES = 4
@@ -27,7 +27,7 @@ SCORE_ORDER = ((0, 0), (1, 0), (0, 1), (0, 2), (1, 1), (1, 2))
 STAGE = N + NQ
 VW_BYTES = F32_BYTES * POOL_PAGES * DV
 VS_ROW = P - 1
-ON_SCALAR = (QT - 1, LAST - 1)
+ON_SCALAR = (QT - 1, 0)
 FLOPS = 2 * NQ * N * (D + DV)
 
 F32 = mybir.dt.float32
@@ -40,7 +40,6 @@ FP8X4 = mybir.dt.float8_e4m3fn_x4
 FP4X4 = mybir.dt.float4_e2m1fn_x4
 ALU = mybir.AluOpType
 ACT = mybir.ActivationFunctionType
-AX = mybir.AxisListType
 
 
 def width(u):
@@ -76,12 +75,13 @@ def tile_attend_pkv4q_soft_cap_sink_kernel(
             return rows.rearrange("f (g x) -> f g x", g=groups)
 
         nc.vector.memset(ks_win[0:KS_ROW0, :].bitcast(I32), 0)
+        nc.vector.memset(ks_win[KS_ROW1:P, :].bitcast(I32), 0)
         nc.vector.memset(vs_win[0:VS_ROW, 0:VS_CUT], 0.0)
 
         nc.sync.dma_start(offs_sb[:], offs)
-        nc.sync.dma_start(ks_win[KS_ROW0:P, :].bitcast(I32), k_scales.rearrange("o f t -> f o t").bitcast(I32))
+        nc.sync.dma_start(ks_win[KS_ROW0:KS_ROW1, :].bitcast(I32), k_scales.rearrange("o f t -> f o t").bitcast(I32))
         nc.scalar.dma_start(
-            stage[KS_ROW0:P, N:STAGE].bitcast(I32), q_scales[0].rearrange("o f q -> f o q").bitcast(I32)
+            stage[KS_ROW0:KS_ROW1, N:STAGE].bitcast(I32), q_scales[0].rearrange("o f q -> f o q").bitcast(I32)
         )
         nc.scalar.dma_start(vs_win[VS_ROW:P, :], vs[0:1, :])
         nc.sync.dma_start(kw_win[:], k_words[0].rearrange("g t b -> g (t b)").bitcast(I32))
@@ -96,7 +96,7 @@ def tile_attend_pkv4q_soft_cap_sink_kernel(
 
         ks_g = keep.tile([P, N], U8, name="ks_g", align_bytes=64)
         nc.vector.tensor_copy(ks_g[:], ks_win[:].indirect(offs_sb[:]))
-        nc.vector.tensor_copy(stage[KS_ROW0:P, 0:N].bitcast(I32), ks_g[KS_ROW0:P, :].bitcast(I32))
+        nc.vector.tensor_copy(stage[KS_ROW0:KS_ROW1, 0:N].bitcast(I32), ks_g[KS_ROW0:KS_ROW1, :].bitcast(I32))
         planes = keep.tile([P, PASSES * STAGE], U8, name="planes", tag="ks_win", align_bytes=64)
         nc.vector.memset(vs_win[0:VS_ROW, VS_CUT:T], 0.0)
         for quad in range(QUADS):
@@ -227,10 +227,6 @@ def tile_attend_pkv4q_soft_cap_sink_kernel(
                         scale=-1.0,
                         accum_out=part[:, c, col + j : col + j + 1],
                     )
-        total = keep.tile([P, QT], F32, name="total")
-        nc.vector.tensor_reduce(total[:], part[:], AX.X, ALU.add)
-        inv = keep.tile([P, QT], F32, name="inv")
-        nc.vector.reciprocal(inv[:], total[:])
 
         w = [keep.tile([P, N], BF16, name=f"w{c}", align_bytes=64) for c in range(QT)]
         for c in range(QT):
@@ -256,15 +252,21 @@ def tile_attend_pkv4q_soft_cap_sink_kernel(
                             ACT.Copy,
                             scale=vs_col[u][:, t : t + 1],
                         )
-                    nc.vector.tensor_copy(
-                        w_page.bitcast(I32).rearrange("p (q h) -> p q h", h=2),
-                        pairs[:].bitcast(I32).rearrange("p (h q) -> p q h", h=2),
+                    nc.scalar.copy(
+                        w_page.bitcast(U32).rearrange("p (q h) -> p q h", h=2),
+                        pairs[:].bitcast(U32).rearrange("p (h q) -> p q h", h=2),
                     )
+
+        total = keep.tile([P, QT], F32, name="total")
+        for c in range(QT):
+            nc.scalar.activation(part[:, c, :], part[:, c, :], ACT.Copy, accum_out=total[:, c : c + 1])
+        inv = keep.tile([P, QT], F32, name="inv")
+        nc.vector.reciprocal(inv[:], total[:])
 
         for c in range(QT):
             wq = keep.tile([P, PAGES * P], U32, name=f"wq{c}", align_bytes=64)
             ws = keep.tile([P, PAGES * P], U8, name=f"ws{c}", align_bytes=64)
-            for lo, hi in ((0, LAST), (LAST, PAGES)) if c == 0 else ((0, 1), (1, PAGES)):
+            for lo, hi in ((0, LAST), (LAST, PAGES)):
                 nc.vector.quantize_mx(
                     out=wq[:, lo * P : hi * P].bitcast(FP8X4),
                     scales=ws[:, lo * P : hi * P],

@@ -21,11 +21,14 @@ KS_ROW0, KS_ROW1 = QUAD, 2 * QUAD
 PAD = 8
 RUN = 8
 F32_BYTES = 4
-WARM_UPS = 2
-VS_CUT = 7 * T // 8
-SCORE_ORDER = ((0, 0), (1, 0), (0, 1), (0, 2), (1, 1), (1, 2))
-STAGE = N + NQ
+HALF = PAGE // 2
+BLOCK = 32
+WARM_UPS = (PAGE, P)
+SCORE_ORDER = tuple((c, u) for u in range(PAGES) for c in range(QT))
+EARLY = NQ + LAST * PAGE
+REST = PAGE + PAGES * DV
 VW_BYTES = F32_BYTES * POOL_PAGES * DV
+EARLY_AT = VW_BYTES - EARLY // 2
 VS_ROW = P - 1
 ON_SCALAR = (QT - 1, 0)
 FLOPS = 2 * NQ * N * (D + DV)
@@ -60,72 +63,80 @@ def tile_attend_pkv4q_soft_cap_sink_kernel(
         offs_sb = keep.tile([P, N // STRIPE], U16, name="offs_sb")
         voffs_sb = keep.tile([P, PAGES * DV // STRIPE], U16, name="voffs_sb")
         ks_win = keep.tile([P, T], U8, name="ks_win", tag="ks_win", align_bytes=64)
+        vsc_win = keep.tile([P, POOL_PAGES * DV], U8, name="vsc_win", align_bytes=64)
         vs_win = keep.tile([P, T], F32, name="vs_win", align_bytes=64)
         kw_win = keep.tile([P, T], I32, name="kw_win", align_bytes=64)
         qw = keep.tile([P, PASSES * NQ], I32, name="qw", align_bytes=64)
-        stage = mid.tile([P, STAGE], U8, name="stage", align_bytes=64, offset=VW_BYTES - STAGE // 2)
-        sink_sb = keep.tile([P, QT], F32, name="sink_sb")
+        early = mid.tile([P, EARLY], U8, name="early", align_bytes=64, offset=EARLY_AT)
+        rest = keep.tile([P, REST], U8, name="rest", align_bytes=64)
         ident = keep.tile([P, P], F32, name="ident", align_bytes=64)
-
-        def page_list(u):
-            return offs_sb[:, u * PAGE // STRIPE : (u + 1) * PAGE // STRIPE]
 
         def plane_rows(plane, quad, groups):
             rows = plane[QUAD * quad : QUAD * quad + ROWS, :].bitcast(I32)
             return rows.rearrange("f (g x) -> f g x", g=groups)
 
+        nc.gpsimd.memset(vsc_win[:].bitcast(I32), 0)
         nc.vector.memset(ks_win[0:KS_ROW0, :].bitcast(I32), 0)
         nc.vector.memset(ks_win[KS_ROW1:P, :].bitcast(I32), 0)
-        nc.vector.memset(vs_win[0:VS_ROW, 0:VS_CUT], 0.0)
+        nc.vector.memset(vs_win[0:VS_ROW, :], 0.0)
 
         nc.sync.dma_start(offs_sb[:], offs)
+        nc.sync.dma_start(voffs_sb[:], voffs)
         nc.sync.dma_start(ks_win[KS_ROW0:KS_ROW1, :].bitcast(I32), k_scales.rearrange("o f t -> f o t").bitcast(I32))
-        nc.scalar.dma_start(
-            stage[KS_ROW0:KS_ROW1, N:STAGE].bitcast(I32), q_scales[0].rearrange("o f q -> f o q").bitcast(I32)
-        )
         nc.scalar.dma_start(vs_win[VS_ROW:P, :], vs[0:1, :])
+        nc.scalar.dma_start(
+            early[KS_ROW0:KS_ROW1, 0:NQ].bitcast(I32), q_scales[0].rearrange("o f q -> f o q").bitcast(I32)
+        )
+        nc.scalar.dma_start(
+            vsc_win[KS_ROW0:KS_ROW1:PASSES, :].bitcast(I32).rearrange("f (u x) -> f u x", u=POOL_PAGES),
+            v_scales.rearrange("u f e -> f u e").bitcast(I32),
+        )
         nc.sync.dma_start(kw_win[:], k_words[0].rearrange("g t b -> g (t b)").bitcast(I32))
         nc.sync.dma_start(
             qw[:].rearrange("g (o q) -> g o q", o=PASSES),
             q_words[0].rearrange("o g q r -> g o (q r)").bitcast(I32),
         )
-        nc.sync.dma_start(voffs_sb[:], voffs)
-        with nc.allow_non_contiguous_dma(reason="one logit a partition"):
-            nc.scalar.dma_start(sink_sb[:], sink[0].rearrange("(c p) o -> p (c o)", p=P))
         make_identity(nc, ident[:])
 
+        vs_g = keep.tile([P, N], F32, name="vs_g", align_bytes=64)
+        nc.scalar.activation(vs_g[:], vs_win[:].indirect(offs_sb[:]), ACT.Copy)
+
+        staged = slice(KS_ROW0, KS_ROW1)
         ks_g = keep.tile([P, N], U8, name="ks_g", align_bytes=64)
         nc.vector.tensor_copy(ks_g[:], ks_win[:].indirect(offs_sb[:]))
-        nc.vector.tensor_copy(stage[KS_ROW0:KS_ROW1, 0:N].bitcast(I32), ks_g[KS_ROW0:KS_ROW1, :].bitcast(I32))
-        planes = keep.tile([P, PASSES * STAGE], U8, name="planes", tag="ks_win", align_bytes=64)
-        nc.vector.memset(vs_win[0:VS_ROW, VS_CUT:T], 0.0)
-        for quad in range(QUADS):
-            first = KS_ROW0 + PASSES * ROWS * quad
-            nc.scalar.dma_start(
-                plane_rows(planes, quad, PASSES),
-                stage[first : first + PASSES * ROWS, :].bitcast(I32),
-            )
+        nc.vector.tensor_copy(early[staged, NQ:EARLY].bitcast(I32), ks_g[staged, 0 : LAST * PAGE].bitcast(I32))
+        vsc_g = keep.tile([P, PAGES * DV], U8, name="vsc_g", align_bytes=64)
+        nc.vector.tensor_copy(vsc_g[:], vsc_win[:].indirect(voffs_sb[:]))
+        nc.vector.tensor_copy(rest[staged, 0:PAGE].bitcast(I32), ks_g[staged, LAST * PAGE : N].bitcast(I32))
+        nc.vector.tensor_copy(rest[staged, PAGE:REST].bitcast(I32), vsc_g[staged, :].bitcast(I32))
+        planes = keep.tile([P, PASSES * (EARLY + REST)], U8, name="planes", tag="ks_win", align_bytes=64)
+        early_planes = planes[:, 0 : PASSES * EARLY]
+        rest_planes = planes[:, PASSES * EARLY : PASSES * (EARLY + REST)]
+        for stage, plane in ((early, early_planes), (rest, rest_planes)):
+            for quad in range(QUADS):
+                first = KS_ROW0 + PASSES * ROWS * quad
+                nc.sync.dma_start(
+                    plane_rows(plane, quad, PASSES),
+                    stage[first : first + PASSES * ROWS, :].bitcast(I32),
+                )
 
-        vs_g = keep.tile([P, N], F32, name="vs_g", align_bytes=64)
-        nc.vector.tensor_copy(vs_g[:], vs_win[:].indirect(offs_sb[:]))
-        vs_col = []
-        for u in range(PAGES):
-            vs_col.append(keep.tile([P, PLACES], F32, name=f"vs_col{u}"))
-            nc.sync.dma_start(vs_col[u][:], vs_g[VS_ROW:P, u * PAGE : (u + 1) * PAGE])
+        def key_plane(o, u, lo, hi):
+            if u == LAST:
+                return rest_planes[:, o * REST + lo : o * REST + hi]
+            return early_planes[:, o * EARLY + NQ + u * PAGE + lo : o * EARLY + NQ + u * PAGE + hi]
 
+        sink_sb = mid.tile([P, QT], F32, name="sink_sb", offset=VW_BYTES)
+        with nc.allow_non_contiguous_dma(reason="one logit a partition"):
+            nc.sync.dma_start(sink_sb[:], sink[0].rearrange("(c p) o -> p (c o)", p=P))
         vw_win = mid.tile([P, POOL_PAGES * DV], I32, name="vw_win", align_bytes=64, offset=0)
         nc.sync.dma_start(
             vw_win[:].rearrange("g (u e) -> g u e", u=POOL_PAGES),
             v_words.rearrange("u g e r -> g u (e r)").bitcast(I32),
         )
-
-        vsc_win = mid.tile([P, POOL_PAGES * DV], U8, name="vsc_win", align_bytes=64, offset=VW_BYTES)
-        nc.gpsimd.memset(vsc_win[:].bitcast(I32), 0)
-        for quad in range(QUADS):
-            nc.sync.dma_start(
-                plane_rows(vsc_win, quad, POOL_PAGES),
-                v_scales[:, ROWS * quad : ROWS * (quad + 1), :].rearrange("u f e -> f u e").bitcast(I32),
-            )
+        vs_col = []
+        for u in range(PAGES):
+            vs_col.append(mid.tile([P, PLACES], F32, name=f"vs_col{u}", offset=VW_BYTES + BLOCK * (u + 1)))
+            nc.sync.dma_start(vs_col[u][:], vs_g[VS_ROW:P, u * PAGE : (u + 1) * PAGE])
 
         th = [
             [
@@ -143,46 +154,46 @@ def tile_attend_pkv4q_soft_cap_sink_kernel(
 
         kp = []
         for u in range(PAGES):
-            kg = ring.tile([P, PAGE], U32, name="kg", align_bytes=64)
-            nc.vector.tensor_copy(kg[:], kw_win[:].bitcast(U32).indirect(page_list(u)))
+            kp.append(keep.tile([P, PASSES, PAGE], U16, name=f"kp{u}", align_bytes=64))
+            kg = []
+            for h in range(2):
+                kg.append(keep.tile([P, HALF], U32, name=f"kg{u}{h}", align_bytes=64))
+                col = (u * PAGE + h * HALF) // STRIPE
+                nc.vector.tensor_copy(
+                    kg[h][:], kw_win[:].bitcast(U32).indirect(offs_sb[:, col : col + HALF // STRIPE])
+                )
             if u == 0:
                 warm = ps_w.tile([P, PAGE], F32, name="warm")
-                for j in range(WARM_UPS):
+                for cols in WARM_UPS:
                     nc.tensor.matmul_mx(
-                        out=warm[:],
+                        out=warm[:, 0:cols],
                         lhsT=qw[:, 0:P].bitcast(FP8X4),
                         lhsT_scale=ks_g[:, 0:P],
-                        rhs=kg[:].bitcast(U16)[:, 0:PAGE].bitcast(FP4X4),
-                        rhs_scale=ks_g[:, 0:PAGE],
+                        rhs=kg[0][:].bitcast(U16)[:, 0:cols].bitcast(FP4X4),
+                        rhs_scale=ks_g[:, 0:cols],
                         start=True,
                         stop=True,
                     )
-            kp.append(ring.tile([P, PASSES * PAGE], U16, name="kp", align_bytes=64))
-            if u == 0:
-                for o in range(PASSES):
-                    nc.vector.tensor_copy(
-                        kp[u][:, o * PAGE : (o + 1) * PAGE],
-                        kg[:].bitcast(U16).rearrange("p (n o) -> p n o", o=PASSES)[:, :, o],
-                    )
-            else:
+            for h in range(2):
                 nc.vector.tensor_copy(
-                    kp[u][:].rearrange("p (o n i) -> p n o i", o=PASSES, i=RUN),
-                    kg[:].bitcast(U16).rearrange("p (n i o) -> p n o i", o=PASSES, i=RUN),
+                    kp[u][:, :, h * HALF : (h + 1) * HALF].rearrange("p o (n i) -> p n o i", i=RUN),
+                    kg[h][:].bitcast(U16).rearrange("p (n i o) -> p n o i", o=PASSES, i=RUN),
                 )
 
         for c, u in SCORE_ORDER:
             scores = ps_w.tile([P, PAGE], F32, name="scores", tag=f"bank{c}{u}")
-            for o in range(PASSES):
-                q_cols = slice(o * NQ + c * P, o * NQ + (c + 1) * P)
-                nc.tensor.matmul_mx(
-                    out=scores[:],
-                    lhsT=qw[:, q_cols].bitcast(FP8X4),
-                    lhsT_scale=planes[:, o * STAGE + N + c * P : o * STAGE + N + (c + 1) * P],
-                    rhs=kp[u][:, o * PAGE : (o + 1) * PAGE].bitcast(FP4X4),
-                    rhs_scale=planes[:, o * STAGE + u * PAGE : o * STAGE + (u + 1) * PAGE],
-                    start=(o == 0),
-                    stop=(o == PASSES - 1),
-                )
+            cuts = (0, HALF, PAGE) if (c, u) == (0, 0) else (0, PAGE)
+            for lo, hi in zip(cuts, cuts[1:]):
+                for o in range(PASSES):
+                    nc.tensor.matmul_mx(
+                        out=scores[:, lo:hi],
+                        lhsT=qw[:, o * NQ + c * P : o * NQ + (c + 1) * P].bitcast(FP8X4),
+                        lhsT_scale=early_planes[:, o * EARLY + c * P : o * EARLY + (c + 1) * P],
+                        rhs=kp[u][:, o, lo:hi].bitcast(FP4X4),
+                        rhs_scale=key_plane(o, u, lo, hi),
+                        start=(o == 0),
+                        stop=(o == PASSES - 1),
+                    )
             nc.scalar.activation(
                 th[c][u][:, 0:PAGE].rearrange("p (t s) -> p t s", t=PLACES),
                 scores[:].rearrange("p (s t) -> p t s", t=PLACES),
@@ -205,8 +216,6 @@ def tile_attend_pkv4q_soft_cap_sink_kernel(
 
         vw_g = late.tile([P, PAGES * DV], U32, name="vw_g", align_bytes=64, offset=0)
         nc.vector.tensor_copy(vw_g[:], vw_win[:].bitcast(U32).indirect(voffs_sb[:]))
-        vsc_g = late.tile([P, PAGES * DV], U8, name="vsc_g", align_bytes=64, offset=F32_BYTES * PAGES * DV)
-        nc.vector.tensor_copy(vsc_g[:], vsc_win[:].indirect(voffs_sb[:]))
 
         prob = [[] for c in range(QT)]
         part = keep.tile([P, QT, PAGES + 1], F32, name="part")
@@ -279,7 +288,7 @@ def tile_attend_pkv4q_soft_cap_sink_kernel(
                     lhsT=wq[:, u * P : (u + 1) * P].bitcast(FP8X4),
                     lhsT_scale=ws[:, u * P : (u + 1) * P],
                     rhs=vw_g[:, u * DV : (u + 1) * DV].bitcast(FP8X4),
-                    rhs_scale=vsc_g[:, u * DV : (u + 1) * DV],
+                    rhs_scale=rest_planes[:, PAGE + u * DV : PAGE + (u + 1) * DV],
                     start=(u == 0),
                     stop=(u == LAST),
                 )

@@ -91,7 +91,9 @@ def tile_attend_pkv4q_soft_cap_sink_kernel(
             vsc_win[KS_ROW0:KS_ROW1:PASSES, :].bitcast(I32).rearrange("f (u x) -> f u x", u=POOL_PAGES),
             v_scales.rearrange("u f e -> f u e").bitcast(I32),
         )
-        nc.sync.dma_start(kw_win[:], k_words[0].rearrange("g t b -> g (t b)").bitcast(I32))
+        k_src = k_words[0].rearrange("g t b -> g (t b)").bitcast(I32)
+        nc.sync.dma_start(kw_win[:, 0 : T // 2], k_src[:, 0 : T // 2])
+        nc.scalar.dma_start(kw_win[:, T // 2 : T], k_src[:, T // 2 : T])
         nc.sync.dma_start(
             qw[:].rearrange("g (o q) -> g o q", o=PASSES),
             q_words[0].rearrange("o g q r -> g o (q r)").bitcast(I32),

@@ -76,9 +76,9 @@ def tile_attend_pkv4q_soft_cap_sink_kernel(
             return rows.rearrange("f (g x) -> f g x", g=groups)
 
         nc.gpsimd.memset(vsc_win[:].bitcast(I32), 0)
+        nc.vector.memset(vs_win[0:VS_ROW, :], 0.0)
         nc.vector.memset(ks_win[0:KS_ROW0, :].bitcast(I32), 0)
         nc.vector.memset(ks_win[KS_ROW1:P, :].bitcast(I32), 0)
-        nc.vector.memset(vs_win[0:VS_ROW, :], 0.0)
 
         nc.sync.dma_start(offs_sb[:], offs)
         nc.sync.dma_start(voffs_sb[:], voffs)

@@ -69,7 +69,6 @@ def tile_attend_pkv4q_soft_cap_sink_kernel(
         qw = keep.tile([P, PASSES * NQ], I32, name="qw", align_bytes=64)
         early = mid.tile([P, EARLY], U8, name="early", align_bytes=64, offset=EARLY_AT)
         rest = keep.tile([P, REST], U8, name="rest", align_bytes=64)
-        ident = keep.tile([P, P], F32, name="ident", align_bytes=64)
 
         def plane_rows(plane, quad, groups):
             rows = plane[QUAD * quad : QUAD * quad + ROWS, :].bitcast(I32)
@@ -98,7 +97,6 @@ def tile_attend_pkv4q_soft_cap_sink_kernel(
             qw[:].rearrange("g (o q) -> g o q", o=PASSES),
             q_words[0].rearrange("o g q r -> g o (q r)").bitcast(I32),
         )
-        make_identity(nc, ident[:])
 
         vs_g = keep.tile([P, N], F32, name="vs_g", align_bytes=64)
         nc.scalar.activation(vs_g[:], vs_win[:].indirect(offs_sb[:]), ACT.Copy)
@@ -159,7 +157,7 @@ def tile_attend_pkv4q_soft_cap_sink_kernel(
             kp.append(keep.tile([P, PASSES, PAGE], U16, name=f"kp{u}", align_bytes=64))
             kg = []
             for h in range(2):
-                kg.append(keep.tile([P, HALF], U32, name=f"kg{u}{h}", align_bytes=64))
+                kg.append(keep.tile([P, HALF], U32, name=f"kg{u}{h}", tag=f"kg{u}{h}", align_bytes=64))
                 col = (u * PAGE + h * HALF) // STRIPE
                 nc.vector.tensor_copy(
                     kg[h][:], kw_win[:].bitcast(U32).indirect(offs_sb[:, col : col + HALF // STRIPE])
@@ -181,6 +179,9 @@ def tile_attend_pkv4q_soft_cap_sink_kernel(
                     kp[u][:, :, h * HALF : (h + 1) * HALF].rearrange("p o (n i) -> p n o i", i=RUN),
                     kg[h][:].bitcast(U16).rearrange("p (n i o) -> p n o i", o=PASSES, i=RUN),
                 )
+
+        ident = keep.tile([P, P], F32, name="ident", tag=f"kg{LAST}1", align_bytes=64)
+        make_identity(nc, ident[:])
 
         for c, u in SCORE_ORDER:
             scores = ps_w.tile([P, PAGE], F32, name="scores", tag=f"bank{c}{u}")

@@ -10,6 +10,7 @@ P = 128
 PLACES = 4
 QUADS = 4
 QUAD = P // QUADS
+QUAD_ORDER = (0, 2, 1, 3)
 ROWS = 4
 STRIPE = 16
 PAGES = N // PAGE
@@ -31,6 +32,9 @@ VW_BYTES = F32_BYTES * POOL_PAGES * DV
 EARLY_AT = VW_BYTES - EARLY // 2
 VS_ROW = P - 1
 ON_SCALAR = (QT - 1, 0)
+LAST_WORDS_AT = EARLY_AT + EARLY
+SINK_AT = LAST_WORDS_AT - BLOCK
+IDENT_AT = LAST_WORDS_AT - F32_BYTES * P // 2
 FLOPS = 2 * NQ * N * (D + DV)
 
 F32 = mybir.dt.float32
@@ -43,10 +47,7 @@ FP8X4 = mybir.dt.float8_e4m3fn_x4
 FP4X4 = mybir.dt.float4_e2m1fn_x4
 ALU = mybir.AluOpType
 ACT = mybir.ActivationFunctionType
-
-
-def width(u):
-    return PAGE + (1 if u == LAST else 0)
+AXIS = mybir.AxisListType
 
 
 def tile_attend_pkv4q_soft_cap_sink_kernel(
@@ -93,7 +94,7 @@ def tile_attend_pkv4q_soft_cap_sink_kernel(
         k_src = k_words[0].rearrange("g t b -> g (t b)").bitcast(I32)
         nc.sync.dma_start(kw_win[:, 0 : T // 2], k_src[:, 0 : T // 2])
         nc.scalar.dma_start(kw_win[:, T // 2 : T], k_src[:, T // 2 : T])
-        nc.sync.dma_start(
+        nc.scalar.dma_start(
             qw[:].rearrange("g (o q) -> g o q", o=PASSES),
             q_words[0].rearrange("o g q r -> g o (q r)").bitcast(I32),
         )
@@ -113,7 +114,7 @@ def tile_attend_pkv4q_soft_cap_sink_kernel(
         early_planes = planes[:, 0 : PASSES * EARLY]
         rest_planes = planes[:, PASSES * EARLY : PASSES * (EARLY + REST)]
         for stage, plane in ((early, early_planes), (rest, rest_planes)):
-            for quad in range(QUADS):
+            for quad in QUAD_ORDER:
                 first = KS_ROW0 + PASSES * ROWS * quad
                 nc.sync.dma_start(
                     plane_rows(plane, quad, PASSES),
@@ -125,7 +126,7 @@ def tile_attend_pkv4q_soft_cap_sink_kernel(
                 return rest_planes[:, o * REST + lo : o * REST + hi]
             return early_planes[:, o * EARLY + NQ + u * PAGE + lo : o * EARLY + NQ + u * PAGE + hi]
 
-        sink_sb = mid.tile([P, QT], F32, name="sink_sb", offset=VW_BYTES)
+        sink_sb = mid.tile([P, QT], F32, name="sink_sb", offset=SINK_AT)
         with nc.allow_non_contiguous_dma(reason="one logit a partition"):
             nc.sync.dma_start(sink_sb[:], sink[0].rearrange("(c p) o -> p (c o)", p=P))
         vw_win = mid.tile([P, POOL_PAGES * DV], I32, name="vw_win", align_bytes=64, offset=0)
@@ -135,21 +136,23 @@ def tile_attend_pkv4q_soft_cap_sink_kernel(
         )
         vs_col = []
         for u in range(PAGES):
-            vs_col.append(mid.tile([P, PLACES], F32, name=f"vs_col{u}", offset=VW_BYTES + BLOCK * (u + 1)))
+            vs_col.append(mid.tile([P, PLACES], F32, name=f"vs_col{u}", offset=VW_BYTES + BLOCK * u))
             nc.sync.dma_start(vs_col[u][:], vs_g[VS_ROW:P, u * PAGE : (u + 1) * PAGE])
 
+        th_apart = [keep.tile([P, PAGE + 2 * PAD], F32, name=f"th_apart{j}", align_bytes=64) for j in range(PAGES + 1)]
+        th_pair = late.tile([P, LAST * PAGE + PAD], F32, name="th_pair", align_bytes=64, offset=0)
         th = [
-            [
-                keep.tile([P, PAGE + PAD], F32, name=f"th{c}{u}", align_bytes=64)
-                for u in range(PAGES)
-                if (c, u) != (QT - 1, LAST)
-            ]
-            for c in range(QT)
+            [th_apart[u][:, 0 : PAGE + PAD + 1] for u in range(PAGES)],
+            [th_apart[PAGES][:, 0:PAGE]] + [th_pair[:, j * PAGE : (j + 1) * PAGE + PAD] for j in range(LAST)],
         ]
-        th[QT - 1].append(late.tile([P, PAGE + PAD], F32, name="th_last", align_bytes=64, offset=0))
         for c in range(QT):
             nc.gpsimd.tensor_scalar(
-                th[c][LAST][:, PAGE : PAGE + 1], sink_sb[:, c : c + 1], 1.0 / CAP, 0.0, ALU.mult, ALU.add
+                th[c][LAST][:, PAGE : PAGE + PAD],
+                sink_sb[:, c : c + 1].to_broadcast([P, PAD]),
+                1.0 / CAP,
+                0.0,
+                ALU.mult,
+                ALU.add,
             )
 
         kp = []
@@ -157,7 +160,10 @@ def tile_attend_pkv4q_soft_cap_sink_kernel(
             kp.append(keep.tile([P, PASSES, PAGE], U16, name=f"kp{u}", align_bytes=64))
             kg = []
             for h in range(2):
-                kg.append(keep.tile([P, HALF], U32, name=f"kg{u}{h}", tag=f"kg{u}{h}", align_bytes=64))
+                if (u, h) == (LAST, 1):
+                    kg.append(mid.tile([P, HALF], U32, name="kg_last", align_bytes=64, offset=LAST_WORDS_AT))
+                else:
+                    kg.append(keep.tile([P, HALF], U32, name=f"kg{u}{h}", align_bytes=64))
                 col = (u * PAGE + h * HALF) // STRIPE
                 nc.vector.tensor_copy(
                     kg[h][:], kw_win[:].bitcast(U32).indirect(offs_sb[:, col : col + HALF // STRIPE])
@@ -180,7 +186,7 @@ def tile_attend_pkv4q_soft_cap_sink_kernel(
                     kg[h][:].bitcast(U16).rearrange("p (n i o) -> p n o i", o=PASSES, i=RUN),
                 )
 
-        ident = keep.tile([P, P], F32, name="ident", tag=f"kg{LAST}1", align_bytes=64)
+        ident = mid.tile([P, P], F32, name="ident", align_bytes=64, offset=IDENT_AT)
         make_identity(nc, ident[:])
 
         for c, u in SCORE_ORDER:
@@ -204,40 +210,43 @@ def tile_attend_pkv4q_soft_cap_sink_kernel(
                 scale=1.0 / CAP,
             )
 
-        neg_c = [keep.tile([P, N + PAD], F32, name=f"neg_c{c}", align_bytes=64) for c in range(QT)]
-        neg_m = [keep.tile([P, PAGES], F32, name=f"neg_m{c}") for c in range(QT)]
-        for c, u in SCORE_ORDER:
-            nc.vector.tensor_scalar(
-                neg_c[c][:, u * PAGE : u * PAGE + width(u)],
-                th[c][u][:, 0 : width(u)],
-                -CAP,
-                neg_m[c][:, u - 1 : u] if u else None,
-                ALU.mult,
-                ALU.min,
-                accum_out=neg_m[c][:, u : u + 1],
-            )
+        neg = [keep.tile([P, PAGE + 2 * PAD], F32, name=f"neg{j}", align_bytes=64) for j in range(PAGES)]
+        neg_pair = keep.tile([P, LAST * PAGE + PAD], F32, name="neg_pair", align_bytes=64)
+        neg_part = [keep.tile([P, 1], F32, name=f"neg_part{c}") for c in range(QT)]
+        neg_m = [keep.tile([P, 1], F32, name=f"neg_m{c}") for c in range(QT)]
+
+        def minimum(target, source, start, result):
+            nc.vector.tensor_scalar(target, source, -CAP, start, ALU.mult, ALU.min, accum_out=result)
+
+        minimum(neg[0][:, 0:PAGE], th[0][0][:, 0:PAGE], None, neg_part[0][:])
+        nc.vector.tensor_reduce(th[0][LAST][:, PAGE + PAD : PAGE + PAD + 1], th[0][1][:, 0:PAGE], AXIS.X, ALU.max)
+        minimum(neg[1][:, 0:PAGE], th[1][0][:, 0:PAGE], None, neg_part[1][:])
+        minimum(neg[2][:, 0 : PAGE + PAD + 1], th[0][LAST], neg_part[0][:], neg_m[0][:])
+        minimum(neg_pair[:, 0 : LAST * PAGE + 1], th_pair[:, 0 : LAST * PAGE + 1], neg_part[1][:], neg_m[1][:])
+        logits = [
+            [(neg[0], -1.0), (th_apart[1], CAP), (neg[2], -1.0)],
+            [(neg[1], -1.0)] + [(neg_pair[:, j * PAGE : LAST * PAGE + 1], -1.0) for j in range(LAST)],
+        ]
 
         vw_g = late.tile([P, PAGES * DV], U32, name="vw_g", align_bytes=64, offset=0)
         nc.vector.tensor_copy(vw_g[:], vw_win[:].bitcast(U32).indirect(voffs_sb[:]))
 
         prob = [[] for c in range(QT)]
-        part = keep.tile([P, QT, PAGES + 1], F32, name="part")
+        part = [keep.tile([P, PAGES + c], F32, name=f"part{c}") for c in range(QT)]
         for c in range(QT):
             for u in range(PAGES):
-                prob[c].append(
-                    keep.tile([P, PAGE + PAD], F32, name=f"prob{c}{u}", tag=f"prob{c}{u}", align_bytes=64)
-                )
-                halved = LAST * c
-                cuts = (0, PAGE // 2, width(u)) if u == halved else (0, width(u))
-                col = u + (u > halved)
+                prob[c].append(keep.tile([P, PAGE + PAD], F32, name=f"prob{c}{u}", align_bytes=64))
+                width = PAGE + (u == LAST)
+                cuts = (0, HALF, width) if (c, u) == (QT - 1, LAST) else (0, width)
+                source, factor = logits[c][u]
                 for j in range(len(cuts) - 1):
                     nc.scalar.activation(
                         prob[c][u][:, cuts[j] : cuts[j + 1]],
-                        neg_c[c][:, u * PAGE + cuts[j] : u * PAGE + cuts[j + 1]],
+                        source[:, cuts[j] : cuts[j + 1]],
                         ACT.Exp,
-                        bias=neg_m[c][:, LAST:PAGES],
-                        scale=-1.0,
-                        accum_out=part[:, c, col + j : col + j + 1],
+                        bias=neg_m[c][:],
+                        scale=factor,
+                        accum_out=part[c][:, u + j : u + j + 1],
                     )
 
         w = [keep.tile([P, N], BF16, name=f"w{c}", align_bytes=64) for c in range(QT)]
@@ -271,7 +280,7 @@ def tile_attend_pkv4q_soft_cap_sink_kernel(
 
         total = keep.tile([P, QT], F32, name="total")
         for c in range(QT):
-            nc.scalar.activation(part[:, c, :], part[:, c, :], ACT.Copy, accum_out=total[:, c : c + 1])
+            nc.scalar.activation(part[c][:], part[c][:], ACT.Copy, accum_out=total[:, c : c + 1])
         inv = keep.tile([P, QT], F32, name="inv")
         nc.vector.reciprocal(inv[:], total[:])
 

@@ -26,8 +26,7 @@ HALF = PAGE // 2
 BLOCK = 32
 WARM_UPS = (PAGE, P)
 SCORE_ORDER = tuple((c, u) for u in range(PAGES) for c in range(QT))
-EARLY = NQ + LAST * PAGE
-REST = PAGE + PAGES * DV
+EARLY = NQ + N
 VW_BYTES = F32_BYTES * POOL_PAGES * DV
 EARLY_AT = VW_BYTES - EARLY // 2
 VS_ROW = P - 1
@@ -64,12 +63,11 @@ def tile_attend_pkv4q_soft_cap_sink_kernel(
         offs_sb = keep.tile([P, N // STRIPE], U16, name="offs_sb")
         voffs_sb = keep.tile([P, PAGES * DV // STRIPE], U16, name="voffs_sb")
         ks_win = keep.tile([P, T], U8, name="ks_win", tag="ks_win", align_bytes=64)
-        vsc_win = keep.tile([P, POOL_PAGES * DV], U8, name="vsc_win", align_bytes=64)
+        vsc_win = keep.tile([P, POOL_PAGES * DV], U8, name="vsc_win", tag="vsc_win", align_bytes=64)
         vs_win = keep.tile([P, T], F32, name="vs_win", align_bytes=64)
         kw_win = keep.tile([P, T], I32, name="kw_win", align_bytes=64)
         qw = keep.tile([P, PASSES * NQ], I32, name="qw", align_bytes=64)
         early = mid.tile([P, EARLY], U8, name="early", align_bytes=64, offset=EARLY_AT)
-        rest = keep.tile([P, REST], U8, name="rest", align_bytes=64)
 
         def plane_rows(plane, quad, groups):
             rows = plane[QUAD * quad : QUAD * quad + ROWS, :].bitcast(I32)
@@ -105,25 +103,18 @@ def tile_attend_pkv4q_soft_cap_sink_kernel(
         staged = slice(KS_ROW0, KS_ROW1)
         ks_g = keep.tile([P, N], U8, name="ks_g", align_bytes=64)
         nc.vector.tensor_copy(ks_g[:], ks_win[:].indirect(offs_sb[:]))
-        nc.vector.tensor_copy(early[staged, NQ:EARLY].bitcast(I32), ks_g[staged, 0 : LAST * PAGE].bitcast(I32))
+        nc.vector.tensor_copy(early[staged, NQ:EARLY].bitcast(I32), ks_g[staged, :].bitcast(I32))
         vsc_g = keep.tile([P, PAGES * DV], U8, name="vsc_g", align_bytes=64)
         nc.vector.tensor_copy(vsc_g[:], vsc_win[:].indirect(voffs_sb[:]))
-        nc.vector.tensor_copy(rest[staged, 0:PAGE].bitcast(I32), ks_g[staged, LAST * PAGE : N].bitcast(I32))
-        nc.vector.tensor_copy(rest[staged, PAGE:REST].bitcast(I32), vsc_g[staged, :].bitcast(I32))
-        planes = keep.tile([P, PASSES * (EARLY + REST)], U8, name="planes", tag="ks_win", align_bytes=64)
-        early_planes = planes[:, 0 : PASSES * EARLY]
-        rest_planes = planes[:, PASSES * EARLY : PASSES * (EARLY + REST)]
-        for stage, plane in ((early, early_planes), (rest, rest_planes)):
-            for quad in QUAD_ORDER:
-                first = KS_ROW0 + PASSES * ROWS * quad
-                nc.sync.dma_start(
-                    plane_rows(plane, quad, PASSES),
-                    stage[first : first + PASSES * ROWS, :].bitcast(I32),
-                )
+        early_planes = keep.tile([P, PASSES * EARLY], U8, name="early_planes", tag="ks_win", align_bytes=64)
+        for quad in QUAD_ORDER:
+            first = KS_ROW0 + PASSES * ROWS * quad
+            nc.sync.dma_start(
+                plane_rows(early_planes, quad, PASSES),
+                early[first : first + PASSES * ROWS, :].bitcast(I32),
+            )
 
         def key_plane(o, u, lo, hi):
-            if u == LAST:
-                return rest_planes[:, o * REST + lo : o * REST + hi]
             return early_planes[:, o * EARLY + NQ + u * PAGE + lo : o * EARLY + NQ + u * PAGE + hi]
 
         sink_sb = mid.tile([P, QT], F32, name="sink_sb", offset=SINK_AT)
@@ -138,6 +129,13 @@ def tile_attend_pkv4q_soft_cap_sink_kernel(
         for u in range(PAGES):
             vs_col.append(mid.tile([P, PLACES], F32, name=f"vs_col{u}", offset=VW_BYTES + BLOCK * u))
             nc.sync.dma_start(vs_col[u][:], vs_g[VS_ROW:P, u * PAGE : (u + 1) * PAGE])
+        value_plane = keep.tile([P, PAGES * DV], U8, name="value_plane", tag="vsc_win", align_bytes=64)
+        for quad in QUAD_ORDER:
+            first = KS_ROW0 + PASSES * ROWS * quad
+            nc.sync.dma_start(
+                value_plane[QUAD * quad : QUAD * quad + ROWS, :].bitcast(I32),
+                vsc_g[first : first + PASSES * ROWS : PASSES, :].bitcast(I32),
+            )
 
         th_apart = [keep.tile([P, PAGE + 2 * PAD], F32, name=f"th_apart{j}", align_bytes=64) for j in range(PAGES + 1)]
         th_pair = late.tile([P, LAST * PAGE + PAD], F32, name="th_pair", align_bytes=64, offset=0)
@@ -300,7 +298,7 @@ def tile_attend_pkv4q_soft_cap_sink_kernel(
                     lhsT=wq[:, u * P : (u + 1) * P].bitcast(FP8X4),
                     lhsT_scale=ws[:, u * P : (u + 1) * P],
                     rhs=vw_g[:, u * DV : (u + 1) * DV].bitcast(FP8X4),
-                    rhs_scale=rest_planes[:, PAGE + u * DV : PAGE + (u + 1) * DV],
+                    rhs_scale=value_plane[:, u * DV : (u + 1) * DV],
                     start=(u == 0),
                     stop=(u == LAST),
                 )

@@ -79,9 +79,9 @@ def tile_attend_pkv4q_soft_cap_sink_kernel(
         nc.vector.memset(ks_win[KS_ROW1:P, :].bitcast(I32), 0)
 
         nc.sync.dma_start(offs_sb[:], offs)
+        nc.sync.dma_start(vs_win[VS_ROW:P, :], vs[0:1, :])
         nc.sync.dma_start(voffs_sb[:], voffs)
-        nc.sync.dma_start(ks_win[KS_ROW0:KS_ROW1, :].bitcast(I32), k_scales.rearrange("o f t -> f o t").bitcast(I32))
-        nc.scalar.dma_start(vs_win[VS_ROW:P, :], vs[0:1, :])
+        nc.scalar.dma_start(ks_win[KS_ROW0:KS_ROW1, :].bitcast(I32), k_scales.rearrange("o f t -> f o t").bitcast(I32))
         nc.scalar.dma_start(
             early[KS_ROW0:KS_ROW1, 0:NQ].bitcast(I32), q_scales[0].rearrange("o f q -> f o q").bitcast(I32)
         )
@@ -92,7 +92,7 @@ def tile_attend_pkv4q_soft_cap_sink_kernel(
         k_src = k_words[0].rearrange("g t b -> g (t b)").bitcast(I32)
         nc.sync.dma_start(kw_win[:, 0 : T // 2], k_src[:, 0 : T // 2])
         nc.scalar.dma_start(kw_win[:, T // 2 : T], k_src[:, T // 2 : T])
-        nc.scalar.dma_start(
+        nc.sync.dma_start(
             qw[:].rearrange("g (o q) -> g o q", o=PASSES),
             q_words[0].rearrange("o g q r -> g o (q r)").bitcast(I32),
         )

@@ -25,7 +25,7 @@ F32_BYTES = 4
 HALF = PAGE // 2
 BLOCK = 32
 WARM_UPS = (PAGE, P)
-SCORE_ORDER = tuple((c, u) for u in range(PAGES) for c in range(QT))
+SCORE_ORDER = ((0, 0), (1, 0), (0, 1), (0, 2), (1, 1), (1, 2))
 EARLY = NQ + N
 VW_BYTES = F32_BYTES * POOL_PAGES * DV
 EARLY_AT = VW_BYTES - EARLY // 2
@@ -137,8 +137,10 @@ def tile_attend_pkv4q_soft_cap_sink_kernel(
                 vsc_g[first : first + PASSES * ROWS : PASSES, :].bitcast(I32),
             )
 
-        th_apart = [keep.tile([P, PAGE + 2 * PAD], F32, name=f"th_apart{j}", align_bytes=64) for j in range(PAGES + 1)]
-        th_pair = late.tile([P, LAST * PAGE + PAD], F32, name="th_pair", align_bytes=64, offset=0)
+        th_apart = [keep.tile([P, PAGE + 2 * PAD], F32, name=f"th_apart{j}", align_bytes=64) for j in range(LAST)]
+        th_apart.append(late.tile([P, PAGE + 2 * PAD], F32, name="th_last", align_bytes=64, offset=0))
+        th_apart.append(keep.tile([P, PAGE + 2 * PAD], F32, name="th_second", align_bytes=64))
+        th_pair = keep.tile([P, LAST * PAGE + PAD], F32, name="th_pair", align_bytes=64)
         th = [
             [th_apart[u][:, 0 : PAGE + PAD + 1] for u in range(PAGES)],
             [th_apart[PAGES][:, 0:PAGE]] + [th_pair[:, j * PAGE : (j + 1) * PAGE + PAD] for j in range(LAST)],
@@ -220,14 +222,13 @@ def tile_attend_pkv4q_soft_cap_sink_kernel(
         nc.vector.tensor_reduce(th[0][LAST][:, PAGE + PAD : PAGE + PAD + 1], th[0][1][:, 0:PAGE], AXIS.X, ALU.max)
         minimum(neg[1][:, 0:PAGE], th[1][0][:, 0:PAGE], None, neg_part[1][:])
         minimum(neg[2][:, 0 : PAGE + PAD + 1], th[0][LAST], neg_part[0][:], neg_m[0][:])
+        vw_g = late.tile([P, PAGES * DV], U32, name="vw_g", align_bytes=64, offset=0)
+        nc.vector.tensor_copy(vw_g[:], vw_win[:].bitcast(U32).indirect(voffs_sb[:]))
         minimum(neg_pair[:, 0 : LAST * PAGE + 1], th_pair[:, 0 : LAST * PAGE + 1], neg_part[1][:], neg_m[1][:])
         logits = [
             [(neg[0], -1.0), (th_apart[1], CAP), (neg[2], -1.0)],
             [(neg[1], -1.0)] + [(neg_pair[:, j * PAGE : LAST * PAGE + 1], -1.0) for j in range(LAST)],
         ]
-
-        vw_g = late.tile([P, PAGES * DV], U32, name="vw_g", align_bytes=64, offset=0)
-        nc.vector.tensor_copy(vw_g[:], vw_win[:].bitcast(U32).indirect(voffs_sb[:]))
 
         prob = [[] for c in range(QT)]
         part = [keep.tile([P, PAGES + c], F32, name=f"part{c}") for c in range(QT)]

@@ -25,7 +25,7 @@ F32_BYTES = 4
 HALF = PAGE // 2
 BLOCK = 32
 WARM_UPS = (PAGE, P)
-SCORE_ORDER = ((0, 0), (1, 0), (0, 1), (0, 2), (1, 1), (1, 2))
+SCORE_ORDER = ((0, 0), (0, 1), (1, 0), (0, 2), (1, 1), (1, 2))
 EARLY = NQ + N
 VW_BYTES = F32_BYTES * POOL_PAGES * DV
 EARLY_AT = VW_BYTES - EARLY // 2
@@ -34,6 +34,7 @@ ON_SCALAR = (QT - 1, 0)
 LAST_WORDS_AT = EARLY_AT + EARLY
 SINK_AT = LAST_WORDS_AT - BLOCK
 IDENT_AT = LAST_WORDS_AT - F32_BYTES * P // 2
+SINK_PAGE = (LAST, 1)
 FLOPS = 2 * NQ * N * (D + DV)
 
 F32 = mybir.dt.float32
@@ -137,17 +138,11 @@ def tile_attend_pkv4q_soft_cap_sink_kernel(
                 vsc_g[first : first + PASSES * ROWS : PASSES, :].bitcast(I32),
             )
 
-        th_apart = [keep.tile([P, PAGE + 2 * PAD], F32, name=f"th_apart{j}", align_bytes=64) for j in range(LAST)]
-        th_apart.append(late.tile([P, PAGE + 2 * PAD], F32, name="th_last", align_bytes=64, offset=0))
-        th_apart.append(keep.tile([P, PAGE + 2 * PAD], F32, name="th_second", align_bytes=64))
-        th_pair = keep.tile([P, LAST * PAGE + PAD], F32, name="th_pair", align_bytes=64)
-        th = [
-            [th_apart[u][:, 0 : PAGE + PAD + 1] for u in range(PAGES)],
-            [th_apart[PAGES][:, 0:PAGE]] + [th_pair[:, j * PAGE : (j + 1) * PAGE + PAD] for j in range(LAST)],
-        ]
+        th = [[keep.tile([P, PAGE + 2 * PAD], F32, name=f"th{c}{u}", align_bytes=64) for u in range(LAST + c)] for c in range(QT)]
+        th[0].append(late.tile([P, PAGE + 2 * PAD], F32, name="th_last", align_bytes=64, offset=0))
         for c in range(QT):
             nc.gpsimd.tensor_scalar(
-                th[c][LAST][:, PAGE : PAGE + PAD],
+                th[c][SINK_PAGE[c]][:, PAGE : PAGE + PAD],
                 sink_sb[:, c : c + 1].to_broadcast([P, PAD]),
                 1.0 / CAP,
                 0.0,
@@ -210,32 +205,37 @@ def tile_attend_pkv4q_soft_cap_sink_kernel(
                 scale=1.0 / CAP,
             )
 
-        neg = [keep.tile([P, PAGE + 2 * PAD], F32, name=f"neg{j}", align_bytes=64) for j in range(PAGES)]
-        neg_pair = keep.tile([P, LAST * PAGE + PAD], F32, name="neg_pair", align_bytes=64)
-        neg_part = [keep.tile([P, 1], F32, name=f"neg_part{c}") for c in range(QT)]
+        behind = [PAGE + PAD, PAGE]
+        neg = [keep.tile([P, behind[c] + LAST], F32, name=f"neg{c}", align_bytes=64) for c in range(QT)]
         neg_m = [keep.tile([P, 1], F32, name=f"neg_m{c}") for c in range(QT)]
 
-        def minimum(target, source, start, result):
-            nc.vector.tensor_scalar(target, source, -CAP, start, ALU.mult, ALU.min, accum_out=result)
+        def largest(c, u):
+            width = PAGE + (u == SINK_PAGE[c])
+            nc.vector.tensor_reduce(
+                th[c][LAST][:, behind[c] + u : behind[c] + u + 1], th[c][u][:, 0:width], AXIS.X, ALU.max
+            )
 
-        minimum(neg[0][:, 0:PAGE], th[0][0][:, 0:PAGE], None, neg_part[0][:])
-        nc.vector.tensor_reduce(th[0][LAST][:, PAGE + PAD : PAGE + PAD + 1], th[0][1][:, 0:PAGE], AXIS.X, ALU.max)
-        minimum(neg[1][:, 0:PAGE], th[1][0][:, 0:PAGE], None, neg_part[1][:])
-        minimum(neg[2][:, 0 : PAGE + PAD + 1], th[0][LAST], neg_part[0][:], neg_m[0][:])
+        def row_maximum(c):
+            nc.vector.tensor_scalar(
+                neg[c][:], th[c][LAST][:, 0 : behind[c] + LAST], -CAP, None, ALU.mult, ALU.min, accum_out=neg_m[c][:]
+            )
+
+        largest(0, 0)
+        largest(0, 1)
+        largest(1, 0)
+        row_maximum(0)
+        largest(1, 1)
         vw_g = late.tile([P, PAGES * DV], U32, name="vw_g", align_bytes=64, offset=0)
         nc.vector.tensor_copy(vw_g[:], vw_win[:].bitcast(U32).indirect(voffs_sb[:]))
-        minimum(neg_pair[:, 0 : LAST * PAGE + 1], th_pair[:, 0 : LAST * PAGE + 1], neg_part[1][:], neg_m[1][:])
-        logits = [
-            [(neg[0], -1.0), (th_apart[1], CAP), (neg[2], -1.0)],
-            [(neg[1], -1.0)] + [(neg_pair[:, j * PAGE : LAST * PAGE + 1], -1.0) for j in range(LAST)],
-        ]
+        row_maximum(1)
+        logits = [[(th[c][u], CAP) for u in range(LAST)] + [(neg[c], -1.0)] for c in range(QT)]
 
         prob = [[] for c in range(QT)]
         part = [keep.tile([P, PAGES + c], F32, name=f"part{c}") for c in range(QT)]
         for c in range(QT):
             for u in range(PAGES):
                 prob[c].append(keep.tile([P, PAGE + PAD], F32, name=f"prob{c}{u}", align_bytes=64))
-                width = PAGE + (u == LAST)
+                width = PAGE + (u == SINK_PAGE[c])
                 cuts = (0, HALF, width) if (c, u) == (QT - 1, LAST) else (0, width)
                 source, factor = logits[c][u]
                 for j in range(len(cuts) - 1):

from contextlib import ExitStack

import concourse.mybir as mybir
from concourse.masks import make_identity

N, T, D, DV, NQ = 1536, 4096, 1024, 128, 256
PAGE = 512
CAP = 2.0
P = 128
PLACES = 4
QUADS = 4
QUAD = P // QUADS
QUAD_ORDER = (0, 2, 1, 3)
ROWS = 4
STRIPE = 16
PAGES = N // PAGE
PASSES = D // PAGE
QT = NQ // P
POOL_PAGES = T // PAGE
LAST = PAGES - 1
KS_ROW0, KS_ROW1 = QUAD, 2 * QUAD
PAD = 8
RUN = 8
F32_BYTES = 4
HALF = PAGE // 2
BLOCK = 32
WARM_UPS = (PAGE, P)
SCORE_ORDER = ((0, 0), (0, 1), (1, 0), (0, 2), (1, 1), (1, 2))
EARLY = NQ + N
VW_BYTES = F32_BYTES * POOL_PAGES * DV
EARLY_AT = VW_BYTES - EARLY // 2
VS_ROW = P - 1
ON_SCALAR = (QT - 1, 0)
LAST_WORDS_AT = EARLY_AT + EARLY
SINK_AT = LAST_WORDS_AT - BLOCK
IDENT_AT = LAST_WORDS_AT - F32_BYTES * P // 2
SINK_PAGE = (LAST, 1)
FLOPS = 2 * NQ * N * (D + DV)

F32 = mybir.dt.float32
BF16 = mybir.dt.bfloat16
I32 = mybir.dt.int32
U32 = mybir.dt.uint32
U16 = mybir.dt.uint16
U8 = mybir.dt.uint8
FP8X4 = mybir.dt.float8_e4m3fn_x4
FP4X4 = mybir.dt.float4_e2m1fn_x4
ALU = mybir.AluOpType
ACT = mybir.ActivationFunctionType
AXIS = mybir.AxisListType


def tile_attend_pkv4q_soft_cap_sink_kernel(
    tc, q_words, q_scales, k_words, k_scales, v_words, v_scales, vs, sink, offs, voffs, out
):
    nc = tc.nc
    with ExitStack() as ctx:
        keep = ctx.enter_context(tc.tile_pool(name="keep", bufs=1))
        ring = ctx.enter_context(tc.tile_pool(name="ring", bufs=PAGES))
        late = ctx.enter_context(tc.tile_pool(name="late", bufs=1))
        mid = ctx.enter_context(tc.tile_pool(name="mid", bufs=1))
        ps_w = ctx.enter_context(tc.psum_pool(name="ps_w", bufs=1))

        offs_sb = keep.tile([P, N // STRIPE], U16, name="offs_sb")
        voffs_sb = keep.tile([P, PAGES * DV // STRIPE], U16, name="voffs_sb")
        ks_win = keep.tile([P, T], U8, name="ks_win", tag="ks_win", align_bytes=64)
        vsc_win = keep.tile([P, POOL_PAGES * DV], U8, name="vsc_win", tag="vsc_win", align_bytes=64)
        vs_win = keep.tile([P, T], F32, name="vs_win", align_bytes=64)
        kw_win = keep.tile([P, T], I32, name="kw_win", align_bytes=64)
        qw = keep.tile([P, PASSES * NQ], I32, name="qw", align_bytes=64)
        early = mid.tile([P, EARLY], U8, name="early", align_bytes=64, offset=EARLY_AT)

        def plane_rows(plane, quad, groups):
            rows = plane[QUAD * quad : QUAD * quad + ROWS, :].bitcast(I32)
            return rows.rearrange("f (g x) -> f g x", g=groups)

        nc.gpsimd.memset(vsc_win[:].bitcast(I32), 0)
        nc.vector.memset(vs_win[0:VS_ROW, :], 0.0)
        nc.vector.memset(ks_win[0:KS_ROW0, :].bitcast(I32), 0)
        nc.vector.memset(ks_win[KS_ROW1:P, :].bitcast(I32), 0)

        nc.sync.dma_start(offs_sb[:], offs)
        nc.sync.dma_start(vs_win[VS_ROW:P, :], vs[0:1, :])
        nc.sync.dma_start(voffs_sb[:], voffs)
        nc.scalar.dma_start(ks_win[KS_ROW0:KS_ROW1, :].bitcast(I32), k_scales.rearrange("o f t -> f o t").bitcast(I32))
        nc.scalar.dma_start(
            early[KS_ROW0:KS_ROW1, 0:NQ].bitcast(I32), q_scales[0].rearrange("o f q -> f o q").bitcast(I32)
        )
        nc.scalar.dma_start(
            vsc_win[KS_ROW0:KS_ROW1:PASSES, :].bitcast(I32).rearrange("f (u x) -> f u x", u=POOL_PAGES),
            v_scales.rearrange("u f e -> f u e").bitcast(I32),
        )
        k_src = k_words[0].rearrange("g t b -> g (t b)").bitcast(I32)
        nc.sync.dma_start(kw_win[:, 0 : T // 2], k_src[:, 0 : T // 2])
        nc.scalar.dma_start(kw_win[:, T // 2 : T], k_src[:, T // 2 : T])
        nc.sync.dma_start(
            qw[:].rearrange("g (o q) -> g o q", o=PASSES),
            q_words[0].rearrange("o g q r -> g o (q r)").bitcast(I32),
        )

        vs_g = keep.tile([P, N], F32, name="vs_g", align_bytes=64)
        nc.scalar.activation(vs_g[:], vs_win[:].indirect(offs_sb[:]), ACT.Copy)

        staged = slice(KS_ROW0, KS_ROW1)
        ks_g = keep.tile([P, N], U8, name="ks_g", align_bytes=64)
        nc.vector.tensor_copy(ks_g[:], ks_win[:].indirect(offs_sb[:]))
        nc.vector.tensor_copy(early[staged, NQ:EARLY].bitcast(I32), ks_g[staged, :].bitcast(I32))
        vsc_g = keep.tile([P, PAGES * DV], U8, name="vsc_g", align_bytes=64)
        nc.vector.tensor_copy(vsc_g[:], vsc_win[:].indirect(voffs_sb[:]))
        early_planes = keep.tile([P, PASSES * EARLY], U8, name="early_planes", tag="ks_win", align_bytes=64)
        for quad in QUAD_ORDER:
            first = KS_ROW0 + PASSES * ROWS * quad
            nc.sync.dma_start(
                plane_rows(early_planes, quad, PASSES),
                early[first : first + PASSES * ROWS, :].bitcast(I32),
            )

        def key_plane(o, u, lo, hi):
            return early_planes[:, o * EARLY + NQ + u * PAGE + lo : o * EARLY + NQ + u * PAGE + hi]

        sink_sb = mid.tile([P, QT], F32, name="sink_sb", offset=SINK_AT)
        with nc.allow_non_contiguous_dma(reason="one logit a partition"):
            nc.sync.dma_start(sink_sb[:], sink[0].rearrange("(c p) o -> p (c o)", p=P))
        vw_win = mid.tile([P, POOL_PAGES * DV], I32, name="vw_win", align_bytes=64, offset=0)
        nc.sync.dma_start(
            vw_win[:].rearrange("g (u e) -> g u e", u=POOL_PAGES),
            v_words.rearrange("u g e r -> g u (e r)").bitcast(I32),
        )
        vs_col = []
        for u in range(PAGES):
            vs_col.append(mid.tile([P, PLACES], F32, name=f"vs_col{u}", offset=VW_BYTES + BLOCK * u))
            nc.sync.dma_start(vs_col[u][:], vs_g[VS_ROW:P, u * PAGE : (u + 1) * PAGE])
        value_plane = keep.tile([P, PAGES * DV], U8, name="value_plane", tag="vsc_win", align_bytes=64)
        for quad in QUAD_ORDER:
            first = KS_ROW0 + PASSES * ROWS * quad
            nc.sync.dma_start(
                value_plane[QUAD * quad : QUAD * quad + ROWS, :].bitcast(I32),
                vsc_g[first : first + PASSES * ROWS : PASSES, :].bitcast(I32),
            )

        th = [[keep.tile([P, PAGE + 2 * PAD], F32, name=f"th{c}{u}", align_bytes=64) for u in range(LAST + c)] for c in range(QT)]
        th[0].append(late.tile([P, PAGE + 2 * PAD], F32, name="th_last", align_bytes=64, offset=0))
        for c in range(QT):
            nc.gpsimd.tensor_scalar(
                th[c][SINK_PAGE[c]][:, PAGE : PAGE + PAD],
                sink_sb[:, c : c + 1].to_broadcast([P, PAD]),
                1.0 / CAP,
                0.0,
                ALU.mult,
                ALU.add,
            )

        kp = []
        for u in range(PAGES):
            kp.append(keep.tile([P, PASSES, PAGE], U16, name=f"kp{u}", align_bytes=64))
            kg = []
            for h in range(2):
                if (u, h) == (LAST, 1):
                    kg.append(mid.tile([P, HALF], U32, name="kg_last", align_bytes=64, offset=LAST_WORDS_AT))
                else:
                    kg.append(keep.tile([P, HALF], U32, name=f"kg{u}{h}", align_bytes=64))
                col = (u * PAGE + h * HALF) // STRIPE
                nc.vector.tensor_copy(
                    kg[h][:], kw_win[:].bitcast(U32).indirect(offs_sb[:, col : col + HALF // STRIPE])
                )
            if u == 0:
                warm = ps_w.tile([P, PAGE], F32, name="warm")
                for cols in WARM_UPS:
                    nc.tensor.matmul_mx(
                        out=warm[:, 0:cols],
                        lhsT=qw[:, 0:P].bitcast(FP8X4),
                        lhsT_scale=ks_g[:, 0:P],
                        rhs=kg[0][:].bitcast(U16)[:, 0:cols].bitcast(FP4X4),
                        rhs_scale=ks_g[:, 0:cols],
                        start=True,
                        stop=True,
                    )
            for h in range(2):
                nc.vector.tensor_copy(
                    kp[u][:, :, h * HALF : (h + 1) * HALF].rearrange("p o (n i) -> p n o i", i=RUN),
                    kg[h][:].bitcast(U16).rearrange("p (n i o) -> p n o i", o=PASSES, i=RUN),
                )

        ident = mid.tile([P, P], F32, name="ident", align_bytes=64, offset=IDENT_AT)
        make_identity(nc, ident[:])

        for c, u in SCORE_ORDER:
            scores = ps_w.tile([P, PAGE], F32, name="scores", tag=f"bank{c}{u}")
            cuts = (0, HALF, PAGE) if (c, u) == (0, 0) else (0, PAGE)
            for lo, hi in zip(cuts, cuts[1:]):
                for o in range(PASSES):
                    nc.tensor.matmul_mx(
                        out=scores[:, lo:hi],
                        lhsT=qw[:, o * NQ + c * P : o * NQ + (c + 1) * P].bitcast(FP8X4),
                        lhsT_scale=early_planes[:, o * EARLY + c * P : o * EARLY + (c + 1) * P],
                        rhs=kp[u][:, o, lo:hi].bitcast(FP4X4),
                        rhs_scale=key_plane(o, u, lo, hi),
                        start=(o == 0),
                        stop=(o == PASSES - 1),
                    )
            nc.scalar.activation(
                th[c][u][:, 0:PAGE].rearrange("p (t s) -> p t s", t=PLACES),
                scores[:].rearrange("p (s t) -> p t s", t=PLACES),
                ACT.Tanh,
                scale=1.0 / CAP,
            )

        behind = [PAGE + PAD, PAGE]
        neg = [keep.tile([P, behind[c] + LAST], F32, name=f"neg{c}", align_bytes=64) for c in range(QT)]
        neg_m = [keep.tile([P, 1], F32, name=f"neg_m{c}") for c in range(QT)]

        def largest(c, u):
            width = PAGE + (u == SINK_PAGE[c])
            nc.vector.tensor_reduce(
                th[c][LAST][:, behind[c] + u : behind[c] + u + 1], th[c][u][:, 0:width], AXIS.X, ALU.max
            )

        def row_maximum(c):
            nc.vector.tensor_scalar(
                neg[c][:], th[c][LAST][:, 0 : behind[c] + LAST], -CAP, None, ALU.mult, ALU.min, accum_out=neg_m[c][:]
            )

        largest(0, 0)
        largest(0, 1)
        largest(1, 0)
        row_maximum(0)
        largest(1, 1)
        vw_g = late.tile([P, PAGES * DV], U32, name="vw_g", align_bytes=64, offset=0)
        nc.vector.tensor_copy(vw_g[:], vw_win[:].bitcast(U32).indirect(voffs_sb[:]))
        row_maximum(1)
        logits = [[(th[c][u], CAP) for u in range(LAST)] + [(neg[c], -1.0)] for c in range(QT)]

        prob = [[] for c in range(QT)]
        part = [keep.tile([P, PAGES + c], F32, name=f"part{c}") for c in range(QT)]
        for c in range(QT):
            for u in range(PAGES):
                prob[c].append(keep.tile([P, PAGE + PAD], F32, name=f"prob{c}{u}", align_bytes=64))
                width = PAGE + (u == SINK_PAGE[c])
                cuts = (0, HALF, width) if (c, u) == (QT - 1, LAST) else (0, width)
                source, factor = logits[c][u]
                for j in range(len(cuts) - 1):
                    nc.scalar.activation(
                        prob[c][u][:, cuts[j] : cuts[j + 1]],
                        source[:, cuts[j] : cuts[j + 1]],
                        ACT.Exp,
                        bias=neg_m[c][:],
                        scale=factor,
                        accum_out=part[c][:, u + j : u + j + 1],
                    )

        w = [keep.tile([P, N], BF16, name=f"w{c}", align_bytes=64) for c in range(QT)]
        for c in range(QT):
            for u in range(PAGES):
                turned = ps_w.tile([P, PAGE], F32, name="turned", tag=f"bank{c}{u}")
                for t in range(PLACES):
                    quarter = slice(t * P, (t + 1) * P)
                    nc.tensor.transpose(turned[:, quarter], prob[c][u][:, quarter], ident[:])
                w_page = w[c][:, u * PAGE : (u + 1) * PAGE]
                if (c, u) != ON_SCALAR:
                    nc.vector.tensor_tensor(
                        w_page.rearrange("p (q t) -> p q t", t=PLACES),
                        turned[:].rearrange("p (t q) -> p q t", t=PLACES),
                        vs_col[u][:].unsqueeze(1).to_broadcast([P, P, PLACES]),
                        ALU.mult,
                    )
                else:
                    pairs = ring.tile([P, PAGE], BF16, name="pairs", align_bytes=64)
                    for t in range(PLACES):
                        nc.scalar.activation(
                            pairs[:].rearrange("p (h q e) -> p h q e", h=2, e=2)[:, t // 2, :, t % 2],
                            turned[:, t * P : (t + 1) * P],
                            ACT.Copy,
                            scale=vs_col[u][:, t : t + 1],
                        )
                    nc.scalar.copy(
                        w_page.bitcast(U32).rearrange("p (q h) -> p q h", h=2),
                        pairs[:].bitcast(U32).rearrange("p (h q) -> p q h", h=2),
                    )

        total = keep.tile([P, QT], F32, name="total")
        for c in range(QT):
            nc.scalar.activation(part[c][:], part[c][:], ACT.Copy, accum_out=total[:, c : c + 1])
        inv = keep.tile([P, QT], F32, name="inv")
        nc.vector.reciprocal(inv[:], total[:])

        for c in range(QT):
            wq = keep.tile([P, PAGES * P], U32, name=f"wq{c}", align_bytes=64)
            ws = keep.tile([P, PAGES * P], U8, name=f"ws{c}", align_bytes=64)
            for lo, hi in ((0, LAST), (LAST, PAGES)):
                nc.vector.quantize_mx(
                    out=wq[:, lo * P : hi * P].bitcast(FP8X4),
                    scales=ws[:, lo * P : hi * P],
                    in_=w[c][:, lo * PAGE : hi * PAGE],
                )
            acc = ps_w.tile([P, DV], F32, name=f"acc{c}", tag=f"bank{QT - 1}{LAST - 1 - c}")
            for u in range(PAGES):
                nc.tensor.matmul_mx(
                    out=acc[:],
                    lhsT=wq[:, u * P : (u + 1) * P].bitcast(FP8X4),
                    lhsT_scale=ws[:, u * P : (u + 1) * P],
                    rhs=vw_g[:, u * DV : (u + 1) * DV].bitcast(FP8X4),
                    rhs_scale=value_plane[:, u * DV : (u + 1) * DV],
                    start=(u == 0),
                    stop=(u == LAST),
                )
            y = keep.tile([P, DV], F32, name=f"y{c}", align_bytes=64)
            nc.scalar.activation(y[:], acc[:], ACT.Copy, scale=inv[:, c : c + 1])
            nc.sync.dma_start(out[0, c * P : (c + 1) * P, :], y[:])
